import numpy as np
import ml_dtypes


def mxq(x, axis, fmt="e4m3"):
    dtype, down = {"e4m3": (ml_dtypes.float8_e4m3fn, 7), "e5m2": (ml_dtypes.float8_e5m2, 14)}[fmt]
    v = np.moveaxis(np.asarray(x, np.float32).astype(ml_dtypes.bfloat16).astype(np.float64), axis, -1)
    blocks = v.reshape(v.shape[:-1] + (-1, 32))
    amax = np.abs(blocks).max(-1, keepdims=True)
    byte = np.maximum(np.where(amax > 0, np.frexp(amax)[1] - 1 + 127, 0) - down, 1)
    scale = np.exp2(byte - 127.0)
    codes = (blocks / scale).astype(np.float32).astype(dtype).astype(np.float64)
    return np.moveaxis((codes * scale).reshape(v.shape), -1, axis)


WIDE = False


def mx_kscale(k):
    if not WIDE:
        return np.ones(k)
    levels = np.array([10, -10, 5, -5, 0])
    if k % 512:
        return np.exp2(np.random.permutation(np.resize(levels, k // 32))).repeat(32)
    a = np.empty((k // 512, 16))
    for p in range(k // 512):
        a[p, :8] = np.random.permutation(np.resize(levels, 8))
        for g in range(8):
            far = levels[np.abs(levels - a[p, g]) >= 10]
            a[p, g + 8] = far[np.random.randint(len(far))]
    return np.exp2(a.ravel()).repeat(32)


BF16 = ml_dtypes.bfloat16


def bf(x):
    return np.asarray(x, np.float32).astype(BF16)


def f64(x):
    return np.asarray(x).astype(np.float64)


E2M1 = np.array([0.0, 0.5, 1.0, 1.5, 2.0, 3.0, 4.0, 6.0, -0.0, -0.5, -1.0, -1.5, -2.0, -3.0, -4.0, -6.0])


def pack_weight(w, fmt):
    k, n = w.shape
    w = f64(bf(w)).reshape(k // 32, 32, n)
    amax = np.abs(w).max(1)
    if fmt == "e4m3":
        byte = np.frexp(amax)[1] - 1 + 127 - 7
    else:
        mant, ex = np.frexp(amax / 6.0)
        byte = np.where(mant > 0.5, ex, ex - 1) + 127
    byte = np.clip(np.where(amax > 0, byte, 1), 1, 254)
    scaled = (w * np.exp2(127.0 - byte)[:, None, :]).reshape(k, n).astype(np.float32)
    by_word = np.ascontiguousarray(scaled.reshape(k // 512, 128, 4, n).transpose(0, 1, 3, 2))
    if fmt == "e4m3":
        words = by_word.astype(ml_dtypes.float8_e4m3fn).view(np.uint8)
    else:
        c = by_word.astype(ml_dtypes.float4_e2m1fn).view(np.uint8) & 0xF
        words = c[..., 0::2] | (c[..., 1::2] << 4)
    return np.ascontiguousarray(words), np.ascontiguousarray(byte.astype(np.uint8).reshape(k // 512, 16, n))


def unpack_weight(words, scales, fmt):
    g, p, n, _ = words.shape
    if fmt == "e4m3":
        vals = np.ascontiguousarray(words).view(ml_dtypes.float8_e4m3fn).astype(np.float64)
    else:
        nib = np.empty((g, p, n, 4), np.uint8)
        nib[..., 0::2] = words & 0xF
        nib[..., 1::2] = words >> 4
        vals = E2M1[nib]
    vals = vals * np.repeat(np.exp2(scales.astype(np.float64) - 127.0), 8, axis=1)[..., None]
    return vals.transpose(0, 1, 3, 2).reshape(g * 512, n)
def pack4(w):
    words, scales = pack_weight(w, "e2m1")
    return words.reshape(words.shape[0], 128, -1), scales


def unpack4(words, scales):
    return unpack_weight(words.reshape(words.shape[0], 128, -1, 2), scales, "e2m1")


B, N, D, M = 4, 1024, 256, 512
M2 = 2 * M


def draw0():
    s, t = mx_kscale(N), mx_kscale(M2)
    v = bf(np.random.standard_normal((B, N, D)) * s[None, :, None])
    enc = np.random.standard_normal((M2, N)) / np.sqrt(N) / s[None, :]
    enc_words, enc_scales = pack4(enc.T)
    dec = np.random.standard_normal((N, M2)) / np.sqrt(M2) / t[None, :]
    dec_words, dec_scales = pack4(dec.T)
    return {"v": v,
            "enc_words": enc_words,
            "enc_scales": enc_scales,
            "dec_words": dec_words,
            "dec_scales": dec_scales,
            "alpha": bf(0.5 + 0.5 * np.random.standard_normal((M, D))),
            "omega": bf(np.random.standard_normal(M)),
            "beta": bf(np.random.standard_normal((M2, D)) * t[:, None])}


def pole_response(alpha, omega):
    s = np.log1p(np.exp(alpha))
    w = omega[:, None]
    den = s * s + w * w
    return s / den, -w / den


def core(v, enc_words, enc_scales, dec_words, dec_scales, alpha, omega, beta):
    m = omega.shape[0]
    c = unpack4(enc_words, enc_scales).T @ mxq(f64(v), 1, "e4m3")
    cr = c[:, :m, :]
    ci = c[:, m:, :]
    hr, hi = pole_response(f64(alpha), f64(omega))
    yr = cr * hr - ci * hi
    yi = cr * hi + ci * hr
    z = np.concatenate([yr, yi], axis=1) * f64(beta)
    return unpack4(dec_words, dec_scales).T @ mxq(z, 1, "e4m3")


def e4m3fn_bytes(y):
    return np.clip(np.asarray(y, np.float64), -448.0, 448.0).astype(np.float32).astype(ml_dtypes.float8_e4m3fn).view(np.uint8)


def e4m3fn_values(b):
    return np.asarray(b, np.uint8).view(ml_dtypes.float8_e4m3fn).astype(np.float64)


def setup_inputs():
    d = draw0()
    x0 = np.asarray(d['v']).astype(np.float64)
    s = (np.max(np.abs(x0), axis=(0, 2), keepdims=True) / 448.0).astype(np.float32)
    out = {}
    for k, v in d.items():
        if k == 'v':
            out['v_bytes'] = e4m3fn_bytes(x0 / s.astype(np.float64))
            out['v_scale'] = s
        else:
            out[k] = v
    return out


def reference(v_bytes, v_scale, enc_words, enc_scales, dec_words, dec_scales, alpha, omega, beta):
    return core(e4m3fn_values(v_bytes) * v_scale.astype(np.float64), enc_words, enc_scales, dec_words, dec_scales, alpha, omega, beta)

@@ -1,0 +1,384 @@
+from contextlib import ExitStack
+
+import concourse.mybir as mybir
+from concourse.masks import make_identity
+
+B, N, D, M = 4, 1024, 256, 512
+M2 = 2 * M
+FLOPS = 2 * 2 * B * N * M2 * D
+
+F32 = mybir.dt.float32
+BF16 = mybir.dt.bfloat16
+I32 = mybir.dt.int32
+U32 = mybir.dt.uint32
+U8 = mybir.dt.uint8
+FP8 = mybir.dt.float8_e4m3fn
+FP8X4 = mybir.dt.float8_e4m3fn_x4
+FP4X4 = mybir.dt.float4_e2m1fn_x4
+ALU = mybir.AluOpType
+ACT = mybir.ActivationFunctionType
+
+P = 128
+PACK = 4
+PASSES = 2
+HALVES = D // P
+TILES = [(0, 0), (1, 0), (0, 1), (1, 1), (2, 0), (2, 1), (3, 0), (3, 1)]
+IL_ON_VECTOR = (4, 6)
+WIDEN_AT = {1: 2, 3: 3}
+EXP_CAP = 30.0
+SQ_ON_SCALAR = 2
+ADD_ENGINE = lambda nc: nc.gpsimd
+
+
+def tile_laplacepoleresidueoperator_w4_kernel(
+    tc, v_bytes, v_scale, enc_words, enc_scales, dec_words, dec_scales, alpha, omega, beta, out
+):
+    nc = tc.nc
+    with ExitStack() as ctx:
+        keep = ctx.enter_context(tc.tile_pool(name="keep", bufs=1))
+        work = ctx.enter_context(tc.tile_pool(name="work", bufs=2))
+        psum = ctx.enter_context(tc.psum_pool(name="psum", bufs=1))
+        ctx.enter_context(tc.manual_schedule())
+
+        def bank(index, shape, dtype, name):
+            return psum.tile(shape, dtype, name=name, tag="bank%d" % index)
+
+        a_bf = keep.tile([P, PACK, D], BF16, name="a_bf")
+        nc.sync.dma_start(out=a_bf[:], in_=alpha.rearrange("(p t) d -> p t d", t=PACK))
+        vs = keep.tile([P, PASSES, PACK], F32, name="vs")
+        nc.sync.dma_start(out=vs[:], in_=v_scale.rearrange("o (g p t) x -> p (o g) (t x)", p=P, t=PACK))
+
+        v_raw = []
+
+        def load_v(b):
+            raw = keep.tile([P, PASSES, PACK * D], U8, name="v_raw%d" % b)
+            nc.sync.dma_start(out=raw[:], in_=v_bytes[b].rearrange("(g p t) d -> p g (t d)", p=P, t=PACK))
+            v_raw.append(raw)
+
+        def load_words(words, name):
+            tile = keep.tile([P, PASSES, 2 * N], U8, name=name, align_bytes=64)
+            nc.sync.dma_start(out=tile[:].bitcast(I32), in_=words.rearrange("g p n -> p g n").bitcast(I32))
+            return tile
+
+        def load_scales(tile, scales):
+            for q in range(4):
+                nc.sync.dma_start(
+                    out=tile[32 * q : 32 * q + 4, :, :].bitcast(I32),
+                    in_=scales[:, 4 * q : 4 * q + 4, :].rearrange("g r n -> r g n").bitcast(I32),
+                )
+
+        enc_s = keep.tile([P, PASSES, M2], U8, name="enc_s", align_bytes=64)
+        dec_s = keep.tile([P, PASSES, N], U8, name="dec_s", align_bytes=64)
+        nc.vector.memset(enc_s[:].bitcast(I32), 0)
+        nc.vector.memset(dec_s[:].bitcast(I32), 0)
+        ident = keep.tile([P, P], F32, name="ident")
+        make_identity(nc, ident[:])
+        ident_bf = keep.tile([P, P], BF16, name="ident_bf")
+        nc.scalar.copy(out=ident_bf[:], in_=ident[:])
+
+        load_v(0)
+        w_bf = keep.tile([P, PACK], BF16, name="w_bf")
+        nc.sync.dma_start(out=w_bf[:], in_=omega.rearrange("(p t) -> p t", t=PACK))
+        beta_bf = keep.tile([P, 2, PACK * D], BF16, name="beta_bf")
+        nc.sync.dma_start(out=beta_bf[:], in_=beta.rearrange("(h p t) d -> p h (t d)", p=P, t=PACK))
+        enc_w = load_words(enc_words, "enc_w")
+        load_scales(enc_s, enc_scales)
+        load_scales(dec_s, dec_scales)
+        load_v(1)
+        load_v(2)
+        load_v(3)
+        dec_w = load_words(dec_words, "dec_w")
+
+        wide = {}
+
+        def widen(b, on_vector):
+            tile = keep.tile([P, PASSES, PACK, D], BF16, name="wide%d" % b)
+            for g in range(PASSES):
+                for t in range(PACK):
+                    src = v_raw[b][:, g, t * D : (t + 1) * D].bitcast(FP8)
+                    if on_vector:
+                        nc.vector.tensor_scalar(
+                            out=tile[:, g, t, :], in0=src, scalar1=vs[:, g, t : t + 1], scalar2=None, op0=ALU.mult
+                        )
+                    else:
+                        nc.scalar.activation(out=tile[:, g, t, :], in_=src, func=ACT.Copy, scale=vs[:, g, t : t + 1])
+            wide[b] = tile
+
+        grouped = {}
+
+        def interleave(j, on_vector):
+            b, dh = TILES[j]
+            tile = work.tile([P, PASSES, P, PACK], BF16, name="v_grouped", align_bytes=64)
+            dst = tile[:].rearrange("p g (c i) t -> p g c t i", i=4)
+            src = wide[b][:, :, :, dh * P : (dh + 1) * P].rearrange("p g t (c i) -> p g c t i", i=4)
+            if on_vector:
+                nc.vector.tensor_copy(out=dst, in_=src)
+            else:
+                nc.scalar.copy(out=dst, in_=src)
+            grouped[j] = tile
+
+        def quantize(src, name, bufs):
+            codes = work.tile([P, PASSES, P], U32, name=name + "_codes", bufs=bufs, align_bytes=64)
+            scales = work.tile([P, PASSES, P], U8, name=name + "_scales", bufs=bufs, align_bytes=64)
+            nc.vector.quantize_mx(
+                out=codes[:].rearrange("p g c -> p (g c)").bitcast(FP8X4),
+                scales=scales[:].rearrange("p g c -> p (g c)"),
+                in_=src[:].rearrange("p g c t -> p (g c t)"),
+            )
+            return codes, scales
+
+        v_mx = {}
+
+        def quantize_v(j):
+            v_mx[j] = quantize(grouped[j], "v", 3)
+
+        c_banks = {}
+
+        def encode(j):
+            codes, scales = v_mx[j]
+            for h in range(2):
+                acc = bank((2 * j + h) % 4, [P, M], F32, "c_acc")
+                for g in range(PASSES):
+                    nc.tensor.matmul_mx(
+                        out=acc[:],
+                        lhsT=codes[:, g, :].bitcast(FP8X4),
+                        lhsT_scale=scales[:, g, :],
+                        rhs=enc_w[:, g, 2 * M * h : 2 * M * (h + 1)].bitcast(FP4X4),
+                        rhs_scale=enc_s[:, g, M * h : M * (h + 1)],
+                        start=(g == 0),
+                        stop=(g == PASSES - 1),
+                    )
+                c_banks[(j, h)] = acc
+
+        terms = {}
+
+        def product(j, z, h):
+            dh = TILES[j][1]
+            tile = work.tile([P, M], F32, name="term%d%d" % (z, h))
+            if z == 0:
+                src = c_banks[(j, h)][:].rearrange("d (p t) -> d t p", t=PACK)
+                view = lambda ap: ap.rearrange("d (t p) -> d t p", t=PACK)
+            else:
+                src = c_banks[(j, h)][:].rearrange("d (p u e) -> d u p e", u=2, e=2)
+                view = lambda ap: ap.rearrange("d (u p e) -> d u p e", u=2, e=2)
+            nc.vector.tensor_tensor(out=view(tile[:]), in0=src, in1=view(coef[(dh, z, h)][:]), op=ALU.mult)
+            terms[(j, z, h)] = tile
+
+        z_im = {}
+
+        def add_imag(j, engine):
+            tile = work.tile([P, M], BF16, name="z_im")
+            engine.tensor_tensor(out=tile[:], in0=terms[(j, 1, 0)][:], in1=terms[(j, 1, 1)][:], op=ALU.add)
+            z_im[j] = tile
+
+        z_bf = {}
+
+        def turn_real(j):
+            tile = work.tile([P, 2, P, PACK], BF16, name="z_bf", align_bytes=64)
+            acc = bank(4, [P, PACK, P], F32, "z_acc")
+            for t in range(PACK):
+                for h in range(2):
+                    nc.tensor.matmul(
+                        out=acc[:, t, :],
+                        lhsT=terms[(j, 0, h)][:, t * P : (t + 1) * P],
+                        rhs=ident[:],
+                        is_transpose=True,
+                        start=(h == 0),
+                        stop=(h == 1),
+                    )
+            nc.scalar.copy(out=tile[:, 0, :, :], in_=acc[:].rearrange("p t d -> p d t"))
+            z_bf[j] = tile
+
+        def turn_imag(j, copy):
+            tile = z_bf[j]
+            pairs = bank(5, [P, 2, P], F32, "z_pairs")
+            words = z_im[j][:].bitcast(F32)
+            for u in range(2):
+                nc.tensor.transpose(pairs[:, u, :], words[:, u * P : (u + 1) * P], ident[:])
+            copy(out=tile[:, 1, :, :].bitcast(F32), in_=pairs[:].rearrange("p u d -> p d u"))
+
+        z_mx = {}
+
+        def quantize_z(j):
+            z_mx[j] = quantize(z_bf[j], "z", 2)
+
+        def decode(j, banks, copies):
+            b, dh = TILES[j]
+            codes, scales = z_mx[j]
+            per_bank = N // P // len(banks)
+            for o, index in enumerate(banks):
+                acc = bank(index, [P, per_bank, P], F32, "o_acc")
+                for i in range(per_bank):
+                    n0 = (per_bank * o + i) * P
+                    for g in range(PASSES):
+                        nc.tensor.matmul_mx(
+                            out=acc[:, i, :],
+                            lhsT=dec_w[:, g, 2 * n0 : 2 * (n0 + P)].bitcast(FP4X4),
+                            lhsT_scale=dec_s[:, g, n0 : n0 + P],
+                            rhs=codes[:, g, :].bitcast(FP8X4),
+                            rhs_scale=scales[:, g, :],
+                            start=(g == 0),
+                            stop=(g == PASSES - 1),
+                        )
+                result = work.tile([P, per_bank, P], F32, name="result", bufs=6)
+                copies[o % len(copies)](out=result[:], in_=acc[:])
+                rows = out[b, per_bank * o * P : per_bank * (o + 1) * P, dh * P : (dh + 1) * P]
+                nc.sync.dma_start(out=rows.rearrange("(i p) d -> p i d", p=P), in_=result[:])
+
+        def turn(slices, index, name):
+            acc = bank(index, [P, PACK, P], F32, name)
+            for t in range(PACK):
+                nc.tensor.transpose(acc[:, t, :], slices[t], ident[:])
+            return acc
+
+        numer = {}
+
+        def turn_numer(dh, z, h, index):
+            if z == h:
+                slices = [beta_s[dh][:, z, t, :] for t in range(PACK)]
+            else:
+                slices = [beta_w[:, z, t, dh * P : (dh + 1) * P] for t in range(PACK)]
+            numer[(dh, z, h)] = turn(slices, index, "numer")
+
+        coef = {}
+
+        def make_coef(dh, z, h):
+            tile = keep.tile([P, M], F32, name="coef%d%d%d" % (dh, z, h))
+            src = numer[(dh, z, h)][:].rearrange("d t p -> d (t p)")
+            if z == 0:
+                nc.vector.tensor_tensor(out=tile[:], in0=src, in1=recip[dh][:], op=ALU.mult)
+            else:
+                turned = lambda ap: ap.rearrange("d (u e p) -> d u p e", u=2, e=2)
+                nc.vector.tensor_tensor(
+                    out=tile[:].rearrange("d (u p e) -> d u p e", u=2, e=2),
+                    in0=turned(src),
+                    in1=turned(recip[dh][:]),
+                    op=ALU.mult,
+                )
+            coef[(dh, z, h)] = tile
+
+        beta_s = {}
+
+        def make_beta_s(dh):
+            tile = keep.tile([P, 2, PACK, P], F32, name="beta_s%d" % dh)
+            cols = slice(dh * P, (dh + 1) * P)
+            nc.vector.tensor_tensor(
+                out=tile[:],
+                in0=beta_bf[:].rearrange("p h (t d) -> p h t d", t=PACK)[:, :, :, cols],
+                in1=soft[:, :, cols].unsqueeze(1).to_broadcast([P, 2, PACK, P]),
+                op=ALU.mult,
+            )
+            beta_s[dh] = tile
+
+        a_cap = keep.tile([P, PACK, D], BF16, name="a_cap")
+        nc.vector.tensor_scalar(out=a_cap[:], in0=a_bf[:], scalar1=EXP_CAP, scalar2=None, op0=ALU.min)
+
+        exp_a = keep.tile([P, PACK, D], F32, name="exp_a")
+        nc.scalar.activation(out=exp_a[:], in_=a_cap[:], func=ACT.Exp)
+        log_a = keep.tile([P, PACK, D], F32, name="log_a")
+        for t in range(PACK):
+            nc.scalar.activation(out=log_a[:, t, :], in_=exp_a[:, t, :], func=ACT.Ln, bias=1.0)
+
+        widen(0, True)
+        w_sq = keep.tile([P, PACK], F32, name="w_sq")
+        nc.vector.tensor_tensor(out=w_sq[:], in0=w_bf[:], in1=w_bf[:], op=ALU.mult)
+        w_signed = keep.tile([P, 2, PACK], F32, name="w_signed")
+        for z, sign in enumerate((1.0, -1.0)):
+            nc.vector.tensor_scalar(out=w_signed[:, z, :], in0=w_bf[:], scalar1=sign, scalar2=None, op0=ALU.mult)
+        interleave(0, True)
+
+        soft = keep.tile([P, PACK, D], F32, name="soft")
+        sq = keep.tile([P, PACK, D], F32, name="sq")
+        log_den = keep.tile([P, PACK, D], F32, name="log_den")
+        for t in range(PACK):
+            nc.vector.tensor_tensor(out=soft[:, t, :], in0=log_a[:, t, :], in1=a_bf[:, t, :], op=ALU.max)
+        for t in range(PACK):
+            if t < SQ_ON_SCALAR:
+                nc.scalar.activation(out=sq[:, t, :], in_=soft[:, t, :], func=ACT.Square)
+            else:
+                nc.vector.tensor_tensor(out=sq[:, t, :], in0=soft[:, t, :], in1=soft[:, t, :], op=ALU.mult)
+        for t in range(PACK):
+            nc.scalar.activation(out=log_den[:, t, :], in_=sq[:, t, :], func=ACT.Ln, bias=w_sq[:, t : t + 1])
+        quantize_v(0)
+        make_beta_s(0)
+        beta_w = keep.tile([P, 2, PACK, D], F32, name="beta_w")
+        for z in range(2):
+            for t in range(PACK):
+                nc.vector.tensor_scalar(
+                    out=beta_w[:, z, t, :],
+                    in0=beta_bf[:, z, t * D : (t + 1) * D],
+                    scalar1=w_signed[:, z, t : t + 1],
+                    scalar2=None,
+                    op0=ALU.mult,
+                )
+        make_beta_s(1)
+        log_den_t = []
+        for dh in range(HALVES):
+            log_den_t.append(turn([log_den[:, t, dh * P : (dh + 1) * P] for t in range(PACK)], 4 + dh, "log_den_t"))
+        turn_numer(0, 0, 0, 2)
+        turn_numer(0, 0, 1, 3)
+        encode(0)
+        turn_numer(0, 1, 0, 6)
+        turn_numer(0, 1, 1, 7)
+
+        recip = {}
+
+        def make_recip(dh):
+            tile = keep.tile([P, M], F32, name="recip%d" % dh)
+            nc.scalar.activation(out=tile[:], in_=log_den_t[dh][:].rearrange("d t p -> d (t p)"), func=ACT.Exp, scale=-1.0)
+            recip[dh] = tile
+
+        make_recip(0)
+        widen(1, False)
+        interleave(1, False)
+        make_recip(1)
+        interleave(2, False)
+
+        count = len(TILES)
+        make_coef(0, 0, 0)
+        make_coef(0, 0, 1)
+        product(0, 0, 0)
+        product(0, 0, 1)
+        turn_real(0)
+        make_coef(0, 1, 0)
+        make_coef(0, 1, 1)
+        turn_numer(1, 1, 0, 6)
+        turn_numer(1, 1, 1, 7)
+        product(0, 1, 0)
+        quantize_v(1)
+        product(0, 1, 1)
+        add_imag(0, ADD_ENGINE(nc))
+        encode(1)
+        make_coef(1, 1, 0)
+        make_coef(1, 1, 1)
+        turn_numer(1, 0, 0, 6)
+        turn_numer(1, 0, 1, 7)
+        for j in range(1, count + 1):
+            if j < count:
+                product(j, 1, 0)
+            if j >= 2:
+                quantize_z(j - 2)
+            if j + 1 < count:
+                quantize_v(j + 1)
+            if j < count:
+                product(j, 1, 1)
+                add_imag(j, ADD_ENGINE(nc))
+                product(j, 0, 0)
+                product(j, 0, 1)
+            if j == 1:
+                make_coef(1, 0, 0)
+                make_coef(1, 0, 1)
+            if 1 <= j - 1 < count:
+                turn_real(j - 1)
+            if j - 1 < count:
+                turn_imag(j - 1, nc.vector.tensor_copy if j == count else nc.scalar.copy)
+            if j + 1 < count:
+                encode(j + 1)
+            if j + 2 < count:
+                interleave(j + 2, j + 2 in IL_ON_VECTOR)
+            if j in WIDEN_AT:
+                widen(WIDEN_AT[j], False)
+            if j >= 2:
+                decode(j - 2, (6, 7), (nc.scalar.copy,))
+        quantize_z(count - 1)
+        decode(count - 1, (0, 1, 2, 3), (nc.vector.tensor_copy, nc.scalar.copy))

@@ -22,12 +22,13 @@ P = 128
 PACK = 4
 PASSES = 2
 HALVES = D // P
-TILES = [(0, 0), (1, 0), (0, 1), (1, 1), (2, 0), (2, 1), (3, 0), (3, 1)]
-IL_ON_VECTOR = (4, 6)
-WIDEN_AT = {1: 2, 3: 3}
-EXP_CAP = 30.0
+TILES = [(b, dh) for dh in range(HALVES) for b in range(B)]
+AHEAD_FROM = 3
+REAL_AS_PAIRS = (4, 5, 6)
+OMEGA_ENGINE = lambda nc, dh, z: nc.gpsimd
+EXP_CAP = 2.0**43
 SQ_ON_SCALAR = 2
-ADD_ENGINE = lambda nc: nc.gpsimd
+EARLY_PLANES = 3
 
 
 def tile_laplacepoleresidueoperator_w4_kernel(
@@ -46,7 +47,10 @@ def tile_laplacepoleresidueoperator_w4_kernel(
         a_bf = keep.tile([P, PACK, D], BF16, name="a_bf")
         nc.sync.dma_start(out=a_bf[:], in_=alpha.rearrange("(p t) d -> p t d", t=PACK))
         vs = keep.tile([P, PASSES, PACK], F32, name="vs")
-        nc.sync.dma_start(out=vs[:], in_=v_scale.rearrange("o (g p t) x -> p (o g) (t x)", p=P, t=PACK))
+        nc.scalar.dma_start(out=vs[:], in_=v_scale.rearrange("o (g p t) x -> p (o g) (t x)", p=P, t=PACK))
+
+        w_bf = keep.tile([P, PACK], BF16, name="w_bf")
+        nc.scalar.dma_start(out=w_bf[:], in_=omega.rearrange("(p t) -> p t", t=PACK))
 
         v_raw = []
 
@@ -77,24 +81,24 @@ def tile_laplacepoleresidueoperator_w4_kernel(
         nc.scalar.copy(out=ident_bf[:], in_=ident[:])
 
         load_v(0)
-        w_bf = keep.tile([P, PACK], BF16, name="w_bf")
-        nc.sync.dma_start(out=w_bf[:], in_=omega.rearrange("(p t) -> p t", t=PACK))
-        beta_bf = keep.tile([P, 2, PACK * D], BF16, name="beta_bf")
-        nc.sync.dma_start(out=beta_bf[:], in_=beta.rearrange("(h p t) d -> p h (t d)", p=P, t=PACK))
+        load_v(1)
+        beta_bf = keep.tile([P, 2, PACK, D], BF16, name="beta_bf")
+        nc.sync.dma_start(out=beta_bf[:], in_=beta.rearrange("(h p t) d -> p h t d", p=P, t=PACK))
         enc_w = load_words(enc_words, "enc_w")
         load_scales(enc_s, enc_scales)
         load_scales(dec_s, dec_scales)
-        load_v(1)
         load_v(2)
         load_v(3)
         dec_w = load_words(dec_words, "dec_w")
 
         wide = {}
 
-        def widen(b, on_vector):
-            tile = keep.tile([P, PASSES, PACK, D], BF16, name="wide%d" % b)
-            for g in range(PASSES):
-                for t in range(PACK):
+        def widen(b, on_vector, planes=range(PASSES * PACK)):
+            if b not in wide:
+                wide[b] = keep.tile([P, PASSES, PACK, D], BF16, name="wide%d" % b)
+            tile = wide[b]
+            for plane in planes:
+                for g, t in [divmod(plane, PACK)]:
                     src = v_raw[b][:, g, t * D : (t + 1) * D].bitcast(FP8)
                     if on_vector:
                         nc.vector.tensor_scalar(
@@ -102,13 +106,12 @@ def tile_laplacepoleresidueoperator_w4_kernel(
                         )
                     else:
                         nc.scalar.activation(out=tile[:, g, t, :], in_=src, func=ACT.Copy, scale=vs[:, g, t : t + 1])
-            wide[b] = tile
 
         grouped = {}
 
         def interleave(j, on_vector):
             b, dh = TILES[j]
-            tile = work.tile([P, PASSES, P, PACK], BF16, name="v_grouped", align_bytes=64)
+            tile = work.tile([P, PASSES, P, PACK], BF16, name="v_grouped", bufs=3, align_bytes=64)
             dst = tile[:].rearrange("p g (c i) t -> p g c t i", i=4)
             src = wide[b][:, :, :, dh * P : (dh + 1) * P].rearrange("p g t (c i) -> p g c t i", i=4)
             if on_vector:
@@ -155,26 +158,31 @@ def tile_laplacepoleresidueoperator_w4_kernel(
         def product(j, z, h):
             dh = TILES[j][1]
             tile = work.tile([P, M], F32, name="term%d%d" % (z, h))
-            if z == 0:
+            factor = coef[(dh, z, h)][:]
+            if z == 0 and j not in REAL_AS_PAIRS:
                 src = c_banks[(j, h)][:].rearrange("d (p t) -> d t p", t=PACK)
-                view = lambda ap: ap.rearrange("d (t p) -> d t p", t=PACK)
+                dst = tile[:].rearrange("d (t p) -> d t p", t=PACK)
+                factor = factor.rearrange("d (t p) -> d t p", t=PACK)
             else:
                 src = c_banks[(j, h)][:].rearrange("d (p u e) -> d u p e", u=2, e=2)
-                view = lambda ap: ap.rearrange("d (u p e) -> d u p e", u=2, e=2)
-            nc.vector.tensor_tensor(out=view(tile[:]), in0=src, in1=view(coef[(dh, z, h)][:]), op=ALU.mult)
+                dst = tile[:].rearrange("d (u p e) -> d u p e", u=2, e=2)
+                if z == 0:
+                    factor = factor.rearrange("d (u e p) -> d u p e", u=2, e=2)
+                else:
+                    factor = factor.rearrange("d (u p e) -> d u p e", u=2, e=2)
+            nc.vector.tensor_tensor(out=dst, in0=src, in1=factor, op=ALU.mult)
             terms[(j, z, h)] = tile
 
-        z_im = {}
+        z_sum = {}
 
-        def add_imag(j, engine):
-            tile = work.tile([P, M], BF16, name="z_im")
-            engine.tensor_tensor(out=tile[:], in0=terms[(j, 1, 0)][:], in1=terms[(j, 1, 1)][:], op=ALU.add)
-            z_im[j] = tile
+        def add_terms(j, z, engine):
+            tile = work.tile([P, M], BF16, name="z_sum%d" % z)
+            engine.tensor_tensor(out=tile[:], in0=terms[(j, z, 0)][:], in1=terms[(j, z, 1)][:], op=ALU.add)
+            z_sum[(j, z)] = tile
 
         z_bf = {}
 
-        def turn_real(j):
-            tile = work.tile([P, 2, P, PACK], BF16, name="z_bf", align_bytes=64)
+        def turn_and_add(j):
             acc = bank(4, [P, PACK, P], F32, "z_acc")
             for t in range(PACK):
                 for h in range(2):
@@ -186,16 +194,21 @@ def tile_laplacepoleresidueoperator_w4_kernel(
                         start=(h == 0),
                         stop=(h == 1),
                     )
-            nc.scalar.copy(out=tile[:, 0, :, :], in_=acc[:].rearrange("p t d -> p d t"))
-            z_bf[j] = tile
+            nc.scalar.copy(out=z_bf[j][:, 0, :, :], in_=acc[:].rearrange("p t d -> p d t"))
 
-        def turn_imag(j, copy):
-            tile = z_bf[j]
-            pairs = bank(5, [P, 2, P], F32, "z_pairs")
-            words = z_im[j][:].bitcast(F32)
+        def turn_pairs(j, z, copy):
+            pairs = bank(4 + z, [P, 2, P], F32, "z_pairs")
+            words = z_sum[(j, z)][:].bitcast(F32)
             for u in range(2):
                 nc.tensor.transpose(pairs[:, u, :], words[:, u * P : (u + 1) * P], ident[:])
-            copy(out=tile[:, 1, :, :].bitcast(F32), in_=pairs[:].rearrange("p u d -> p d u"))
+            copy(out=z_bf[j][:, z, :, :].bitcast(F32), in_=pairs[:].rearrange("p u d -> p d u"))
+
+        def turn_real(j):
+            z_bf[j] = work.tile([P, 2, P, PACK], BF16, name="z_bf", align_bytes=64)
+            if j in REAL_AS_PAIRS:
+                turn_pairs(j, 0, nc.scalar.copy)
+            else:
+                turn_and_add(j)
 
         z_mx = {}
 
@@ -231,61 +244,71 @@ def tile_laplacepoleresidueoperator_w4_kernel(
                 nc.tensor.transpose(acc[:, t, :], slices[t], ident[:])
             return acc
 
-        numer = {}
+        turned = {}
 
-        def turn_numer(dh, z, h, index):
-            if z == h:
-                slices = [beta_s[dh][:, z, t, :] for t in range(PACK)]
-            else:
-                slices = [beta_w[:, z, t, dh * P : (dh + 1) * P] for t in range(PACK)]
-            numer[(dh, z, h)] = turn(slices, index, "numer")
+        def turn_inputs(dh):
+            cols = slice(dh * P, (dh + 1) * P)
+            acc = bank(6, [P, 2, PACK, P], BF16, "beta_t")
+            for z in range(2):
+                for t in range(PACK):
+                    nc.tensor.transpose(acc[:, z, t, :], beta_bf[:, z, t, cols], ident_bf[:])
+            turned[dh] = (acc, turn([soft[:, t, cols] for t in range(PACK)], 7, "soft_t"))
 
+        def in_order(ap, z):
+            if z == 0:
+                return ap
+            return ap.rearrange("d (u e) p -> d u p e", u=2)
+
+        def as_order(ap, z):
+            if z == 0:
+                return ap.rearrange("d (t p) -> d t p", t=PACK)
+            return ap.rearrange("d (u p e) -> d u p e", u=2, e=2)
+
+        gain = {}
         coef = {}
 
-        def make_coef(dh, z, h):
-            tile = keep.tile([P, M], F32, name="coef%d%d%d" % (dh, z, h))
-            src = numer[(dh, z, h)][:].rearrange("d t p -> d (t p)")
-            if z == 0:
-                nc.vector.tensor_tensor(out=tile[:], in0=src, in1=recip[dh][:], op=ALU.mult)
-            else:
-                turned = lambda ap: ap.rearrange("d (u e p) -> d u p e", u=2, e=2)
-                nc.vector.tensor_tensor(
-                    out=tile[:].rearrange("d (u p e) -> d u p e", u=2, e=2),
-                    in0=turned(src),
-                    in1=turned(recip[dh][:]),
-                    op=ALU.mult,
-                )
-            coef[(dh, z, h)] = tile
-
-        beta_s = {}
-
-        def make_beta_s(dh):
-            tile = keep.tile([P, 2, PACK, P], F32, name="beta_s%d" % dh)
-            cols = slice(dh * P, (dh + 1) * P)
+        def make_gain(dh, z):
+            tile = keep.tile([P, M], F32, name="gain%d%d" % (dh, z))
             nc.vector.tensor_tensor(
-                out=tile[:],
-                in0=beta_bf[:].rearrange("p h (t d) -> p h t d", t=PACK)[:, :, :, cols],
-                in1=soft[:, :, cols].unsqueeze(1).to_broadcast([P, 2, PACK, P]),
+                out=as_order(tile[:], z),
+                in0=in_order(turned[dh][0][:, z, :, :], z),
+                in1=in_order(recip[dh][:], z),
                 op=ALU.mult,
             )
-            beta_s[dh] = tile
+            gain[(dh, z)] = tile
 
-        a_cap = keep.tile([P, PACK, D], BF16, name="a_cap")
-        nc.vector.tensor_scalar(out=a_cap[:], in0=a_bf[:], scalar1=EXP_CAP, scalar2=None, op0=ALU.min)
+        def make_coef_soft(dh, z):
+            tile = keep.tile([P, M], F32, name="coef%d%d%d" % (dh, z, z))
+            nc.vector.tensor_tensor(
+                out=as_order(tile[:], z), in0=in_order(turned[dh][1][:], z), in1=as_order(gain[(dh, z)][:], z), op=ALU.mult
+            )
+            coef[(dh, z, z)] = tile
+
+        def make_coef_omega(dh, z):
+            tile = keep.tile([P, M], F32, name="coef%d%d%d" % (dh, z, 1 - z))
+            OMEGA_ENGINE(nc, dh, z).tensor_tensor(out=tile[:], in0=gain[(dh, z)][:], in1=w_rows[:, z, :], op=ALU.mult)
+            coef[(dh, z, 1 - z)] = tile
 
         exp_a = keep.tile([P, PACK, D], F32, name="exp_a")
-        nc.scalar.activation(out=exp_a[:], in_=a_cap[:], func=ACT.Exp)
-        log_a = keep.tile([P, PACK, D], F32, name="log_a")
-        for t in range(PACK):
-            nc.scalar.activation(out=log_a[:, t, :], in_=exp_a[:, t, :], func=ACT.Ln, bias=1.0)
-
-        widen(0, True)
+        nc.scalar.activation(out=exp_a[:], in_=a_bf[:], func=ACT.Exp)
         w_sq = keep.tile([P, PACK], F32, name="w_sq")
         nc.vector.tensor_tensor(out=w_sq[:], in0=w_bf[:], in1=w_bf[:], op=ALU.mult)
-        w_signed = keep.tile([P, 2, PACK], F32, name="w_signed")
-        for z, sign in enumerate((1.0, -1.0)):
-            nc.vector.tensor_scalar(out=w_signed[:, z, :], in0=w_bf[:], scalar1=sign, scalar2=None, op0=ALU.mult)
-        interleave(0, True)
+        w_neg = keep.tile([P, PACK], BF16, name="w_neg")
+        nc.vector.tensor_scalar(out=w_neg[:], in0=w_bf[:], scalar1=-1.0, scalar2=None, op0=ALU.mult)
+        widen(0, True, range(EARLY_PLANES))
+        exp_cap = keep.tile([P, PACK, D], F32, name="exp_cap")
+        nc.vector.tensor_scalar(out=exp_cap[:], in0=exp_a[:], scalar1=EXP_CAP, scalar2=None, op0=ALU.min)
+        w_acc = bank(3, [P, 2, PACK, P], BF16, "w_acc")
+        for z, col in enumerate((w_bf, w_neg)):
+            for t in range(PACK):
+                nc.tensor.matmul(
+                    out=w_acc[:, z, t, :], lhsT=col[:, t : t + 1].to_broadcast([P, P]), rhs=ident_bf[:], start=True, stop=True
+                )
+
+        widen(0, True, range(EARLY_PLANES, PASSES * PACK))
+        log_a = keep.tile([P, PACK, D], F32, name="log_a")
+        for t in range(PACK):
+            nc.scalar.activation(out=log_a[:, t, :], in_=exp_cap[:, t, :], func=ACT.Ln, bias=1.0)
 
         soft = keep.tile([P, PACK, D], F32, name="soft")
         sq = keep.tile([P, PACK, D], F32, name="sq")
@@ -299,85 +322,78 @@ def tile_laplacepoleresidueoperator_w4_kernel(
                 nc.vector.tensor_tensor(out=sq[:, t, :], in0=soft[:, t, :], in1=soft[:, t, :], op=ALU.mult)
         for t in range(PACK):
             nc.scalar.activation(out=log_den[:, t, :], in_=sq[:, t, :], func=ACT.Ln, bias=w_sq[:, t : t + 1])
+        widen(1, True)
+        interleave(0, True)
+        interleave(1, True)
         quantize_v(0)
-        make_beta_s(0)
-        beta_w = keep.tile([P, 2, PACK, D], F32, name="beta_w")
-        for z in range(2):
-            for t in range(PACK):
-                nc.vector.tensor_scalar(
-                    out=beta_w[:, z, t, :],
-                    in0=beta_bf[:, z, t * D : (t + 1) * D],
-                    scalar1=w_signed[:, z, t : t + 1],
-                    scalar2=None,
-                    op0=ALU.mult,
-                )
-        make_beta_s(1)
+        quantize_v(1)
+        turn_inputs(0)
         log_den_t = []
         for dh in range(HALVES):
             log_den_t.append(turn([log_den[:, t, dh * P : (dh + 1) * P] for t in range(PACK)], 4 + dh, "log_den_t"))
-        turn_numer(0, 0, 0, 2)
-        turn_numer(0, 0, 1, 3)
         encode(0)
-        turn_numer(0, 1, 0, 6)
-        turn_numer(0, 1, 1, 7)
 
         recip = {}
 
         def make_recip(dh):
-            tile = keep.tile([P, M], F32, name="recip%d" % dh)
-            nc.scalar.activation(out=tile[:], in_=log_den_t[dh][:].rearrange("d t p -> d (t p)"), func=ACT.Exp, scale=-1.0)
+            tile = keep.tile([P, PACK, P], F32, name="recip%d" % dh)
+            nc.scalar.activation(out=tile[:], in_=log_den_t[dh][:], func=ACT.Exp, scale=-1.0)
             recip[dh] = tile
 
         make_recip(0)
-        widen(1, False)
-        interleave(1, False)
+        w_rows = keep.tile([P, 2, M], BF16, name="w_rows")
+        for z in range(2):
+            nc.scalar.copy(out=as_order(w_rows[:, z, :], z), in_=in_order(w_acc[:, z, :, :], z))
         make_recip(1)
+        widen(2, False)
         interleave(2, False)
+        widen(3, False)
 
         count = len(TILES)
-        make_coef(0, 0, 0)
-        make_coef(0, 0, 1)
+        for z in (1, 0):
+            make_gain(0, z)
+            make_coef_omega(0, z)
+        encode(1)
+        make_coef_soft(0, 1)
+        product(0, 1, 1)
+        make_coef_soft(0, 0)
+        turn_inputs(1)
+        product(0, 1, 0)
+        add_terms(0, 1, nc.gpsimd)
         product(0, 0, 0)
         product(0, 0, 1)
-        turn_real(0)
-        make_coef(0, 1, 0)
-        make_coef(0, 1, 1)
-        turn_numer(1, 1, 0, 6)
-        turn_numer(1, 1, 1, 7)
-        product(0, 1, 0)
-        quantize_v(1)
-        product(0, 1, 1)
-        add_imag(0, ADD_ENGINE(nc))
-        encode(1)
-        make_coef(1, 1, 0)
-        make_coef(1, 1, 1)
-        turn_numer(1, 0, 0, 6)
-        turn_numer(1, 0, 1, 7)
         for j in range(1, count + 1):
             if j < count:
                 product(j, 1, 0)
+            if j - 1 in REAL_AS_PAIRS:
+                add_terms(j - 1, 0, nc.vector)
             if j >= 2:
                 quantize_z(j - 2)
-            if j + 1 < count:
+            if j <= AHEAD_FROM:
                 quantize_v(j + 1)
+            if AHEAD_FROM <= j < count - 2:
+                quantize_v(j + 2)
             if j < count:
                 product(j, 1, 1)
-                add_imag(j, ADD_ENGINE(nc))
+                add_terms(j, 1, nc.gpsimd)
+                if j == 1:
+                    make_gain(1, 1)
+                    make_coef_omega(1, 1)
+                    make_gain(1, 0)
+                if j == 2:
+                    make_coef_omega(1, 0)
+                    make_coef_soft(1, 1)
+                    make_coef_soft(1, 0)
                 product(j, 0, 0)
                 product(j, 0, 1)
-            if j == 1:
-                make_coef(1, 0, 0)
-                make_coef(1, 0, 1)
-            if 1 <= j - 1 < count:
-                turn_real(j - 1)
-            if j - 1 < count:
-                turn_imag(j - 1, nc.vector.tensor_copy if j == count else nc.scalar.copy)
+            turn_real(j - 1)
+            turn_pairs(j - 1, 1, nc.vector.tensor_copy if j == count else nc.scalar.copy)
             if j + 1 < count:
                 encode(j + 1)
-            if j + 2 < count:
-                interleave(j + 2, j + 2 in IL_ON_VECTOR)
-            if j in WIDEN_AT:
-                widen(WIDEN_AT[j], False)
+            if j < AHEAD_FROM:
+                interleave(j + 2, False)
+            if AHEAD_FROM - 1 <= j < count - 3:
+                interleave(j + 3, False)
             if j >= 2:
                 decode(j - 2, (6, 7), (nc.scalar.copy,))
         quantize_z(count - 1)

@@ -45,12 +45,11 @@ def tile_laplacepoleresidueoperator_w4_kernel(
             return psum.tile(shape, dtype, name=name, tag="bank%d" % index)
 
         a_bf = keep.tile([P, PACK, D], BF16, name="a_bf")
-        nc.sync.dma_start(out=a_bf[:], in_=alpha.rearrange("(p t) d -> p t d", t=PACK))
+        for u in range(2):
+            nc.sync.dma_start(out=a_bf[:, 2 * u : 2 * u + 2, :], in_=alpha.rearrange("(p t) d -> p t d", t=PACK)[:, 2 * u : 2 * u + 2, :])
         vs = keep.tile([P, PASSES, PACK], F32, name="vs")
-        nc.scalar.dma_start(out=vs[:], in_=v_scale.rearrange("o (g p t) x -> p (o g) (t x)", p=P, t=PACK))
+        nc.sync.dma_start(out=vs[:], in_=v_scale.rearrange("o (g p t) x -> p (o g) (t x)", p=P, t=PACK))
 
-        w_bf = keep.tile([P, PACK], BF16, name="w_bf")
-        nc.scalar.dma_start(out=w_bf[:], in_=omega.rearrange("(p t) -> p t", t=PACK))
 
         v_raw = []
 
@@ -73,14 +72,17 @@ def tile_laplacepoleresidueoperator_w4_kernel(
 
         enc_s = keep.tile([P, PASSES, M2], U8, name="enc_s", align_bytes=64)
         dec_s = keep.tile([P, PASSES, N], U8, name="dec_s", align_bytes=64)
+        ident = keep.tile([P, P], F32, name="ident")
+        nc.vector.memset(ident[:], 0.0)
+        make_identity(nc, ident[:], nomemset=True)
         nc.vector.memset(enc_s[:].bitcast(I32), 0)
         nc.vector.memset(dec_s[:].bitcast(I32), 0)
-        ident = keep.tile([P, P], F32, name="ident")
-        make_identity(nc, ident[:])
         ident_bf = keep.tile([P, P], BF16, name="ident_bf")
         nc.scalar.copy(out=ident_bf[:], in_=ident[:])
 
         load_v(0)
+        w_bf = keep.tile([P, PACK], BF16, name="w_bf")
+        nc.sync.dma_start(out=w_bf[:], in_=omega.rearrange("(p t) -> p t", t=PACK))
         load_v(1)
         beta_bf = keep.tile([P, 2, PACK, D], BF16, name="beta_bf")
         nc.sync.dma_start(out=beta_bf[:], in_=beta.rearrange("(h p t) d -> p h t d", p=P, t=PACK))
@@ -244,6 +246,11 @@ def tile_laplacepoleresidueoperator_w4_kernel(
                 nc.tensor.transpose(acc[:, t, :], slices[t], ident[:])
             return acc
 
+        def keep_warm(index, passes):
+            acc = bank(index, [P, M], F32, "warm")
+            for i in range(passes):
+                nc.tensor.matmul(out=acc[:], lhsT=ident_bf[:], rhs=beta_bf[:, 0, 0:2, :].rearrange("p t d -> p (t d)"), start=True, stop=True)
+
         turned = {}
 
         def turn_inputs(dh):
@@ -290,14 +297,15 @@ def tile_laplacepoleresidueoperator_w4_kernel(
             coef[(dh, z, 1 - z)] = tile
 
         exp_a = keep.tile([P, PACK, D], F32, name="exp_a")
-        nc.scalar.activation(out=exp_a[:], in_=a_bf[:], func=ACT.Exp)
+        for u in range(2):
+            nc.scalar.activation(out=exp_a[:, 2 * u : 2 * u + 2, :], in_=a_bf[:, 2 * u : 2 * u + 2, :], func=ACT.Exp)
+        widen(0, True, range(EARLY_PLANES))
+        exp_cap = keep.tile([P, PACK, D], F32, name="exp_cap")
+        nc.vector.tensor_scalar(out=exp_cap[:], in0=exp_a[:], scalar1=EXP_CAP, scalar2=None, op0=ALU.min)
         w_sq = keep.tile([P, PACK], F32, name="w_sq")
         nc.vector.tensor_tensor(out=w_sq[:], in0=w_bf[:], in1=w_bf[:], op=ALU.mult)
         w_neg = keep.tile([P, PACK], BF16, name="w_neg")
         nc.vector.tensor_scalar(out=w_neg[:], in0=w_bf[:], scalar1=-1.0, scalar2=None, op0=ALU.mult)
-        widen(0, True, range(EARLY_PLANES))
-        exp_cap = keep.tile([P, PACK, D], F32, name="exp_cap")
-        nc.vector.tensor_scalar(out=exp_cap[:], in0=exp_a[:], scalar1=EXP_CAP, scalar2=None, op0=ALU.min)
         w_acc = bank(3, [P, 2, PACK, P], BF16, "w_acc")
         for z, col in enumerate((w_bf, w_neg)):
             for t in range(PACK):
@@ -331,6 +339,7 @@ def tile_laplacepoleresidueoperator_w4_kernel(
         log_den_t = []
         for dh in range(HALVES):
             log_den_t.append(turn([log_den[:, t, dh * P : (dh + 1) * P] for t in range(PACK)], 4 + dh, "log_den_t"))
+        keep_warm(2, 4)
         encode(0)
 
         recip = {}
@@ -358,6 +367,7 @@ def tile_laplacepoleresidueoperator_w4_kernel(
         product(0, 1, 1)
         make_coef_soft(0, 0)
         turn_inputs(1)
+        keep_warm(5, 4)
         product(0, 1, 0)
         add_terms(0, 1, nc.gpsimd)
         product(0, 0, 0)
@@ -386,8 +396,12 @@ def tile_laplacepoleresidueoperator_w4_kernel(
                     make_coef_soft(1, 0)
                 product(j, 0, 0)
                 product(j, 0, 1)
+            if j == 2:
+                keep_warm(6, 4)
             turn_real(j - 1)
             turn_pairs(j - 1, 1, nc.vector.tensor_copy if j == count else nc.scalar.copy)
+            if j in (2, 3):
+                keep_warm(6, 2)
             if j + 1 < count:
                 encode(j + 1)
             if j < AHEAD_FROM:

@@ -26,9 +26,10 @@ TILES = [(b, dh) for dh in range(HALVES) for b in range(B)]
 AHEAD_FROM = 3
 REAL_AS_PAIRS = (4, 5, 6)
 OMEGA_ENGINE = lambda nc, dh, z: nc.gpsimd
-EXP_CAP = 2.0**43
+LOG_CAP = 40.0
 SQ_ON_SCALAR = 2
-EARLY_PLANES = 3
+FINE_FROM = 7
+EARLY_PLANES = 2
 
 
 def tile_laplacepoleresidueoperator_w4_kernel(
@@ -120,6 +121,21 @@ def tile_laplacepoleresidueoperator_w4_kernel(
                 nc.vector.tensor_copy(out=dst, in_=src)
             else:
                 nc.scalar.copy(out=dst, in_=src)
+            grouped[j] = tile
+
+        def interleave_on_tensor(j, index):
+            b, dh = TILES[j]
+            tile = work.tile([P, PASSES, P, PACK], BF16, name="v_grouped", bufs=3, align_bytes=64)
+            acc = bank(index, [P, PASSES, P, PACK], BF16, "v_acc")
+            for g in range(PASSES):
+                nc.tensor.matmul(
+                    out=acc[:, g, :, :],
+                    lhsT=ident_bf[:],
+                    rhs=wide[b][:, g, :, dh * P : (dh + 1) * P].rearrange("p t c -> p c t"),
+                    start=True,
+                    stop=True,
+                )
+            nc.scalar.copy(out=tile[:], in_=acc[:])
             grouped[j] = tile
 
         def quantize(src, name, bufs):
@@ -235,7 +251,7 @@ def tile_laplacepoleresidueoperator_w4_kernel(
                             start=(g == 0),
                             stop=(g == PASSES - 1),
                         )
-                result = work.tile([P, per_bank, P], F32, name="result", bufs=6)
+                result = work.tile([P, per_bank, P], F32, name="result", bufs=8)
                 copies[o % len(copies)](out=result[:], in_=acc[:])
                 rows = out[b, per_bank * o * P : per_bank * (o + 1) * P, dh * P : (dh + 1) * P]
                 nc.sync.dma_start(out=rows.rearrange("(i p) d -> p i d", p=P), in_=result[:])
@@ -299,9 +315,7 @@ def tile_laplacepoleresidueoperator_w4_kernel(
         exp_a = keep.tile([P, PACK, D], F32, name="exp_a")
         for u in range(2):
             nc.scalar.activation(out=exp_a[:, 2 * u : 2 * u + 2, :], in_=a_bf[:, 2 * u : 2 * u + 2, :], func=ACT.Exp)
-        widen(0, True, range(EARLY_PLANES))
-        exp_cap = keep.tile([P, PACK, D], F32, name="exp_cap")
-        nc.vector.tensor_scalar(out=exp_cap[:], in0=exp_a[:], scalar1=EXP_CAP, scalar2=None, op0=ALU.min)
+        widen(0, True)
         w_sq = keep.tile([P, PACK], F32, name="w_sq")
         nc.vector.tensor_tensor(out=w_sq[:], in0=w_bf[:], in1=w_bf[:], op=ALU.mult)
         w_neg = keep.tile([P, PACK], BF16, name="w_neg")
@@ -313,16 +327,18 @@ def tile_laplacepoleresidueoperator_w4_kernel(
                     out=w_acc[:, z, t, :], lhsT=col[:, t : t + 1].to_broadcast([P, P]), rhs=ident_bf[:], start=True, stop=True
                 )
 
-        widen(0, True, range(EARLY_PLANES, PASSES * PACK))
         log_a = keep.tile([P, PACK, D], F32, name="log_a")
         for t in range(PACK):
-            nc.scalar.activation(out=log_a[:, t, :], in_=exp_cap[:, t, :], func=ACT.Ln, bias=1.0)
+            nc.scalar.activation(out=log_a[:, t, :], in_=exp_a[:, t, :], func=ACT.Ln, bias=1.0)
 
+        widen(1, True, range(EARLY_PLANES))
         soft = keep.tile([P, PACK, D], F32, name="soft")
         sq = keep.tile([P, PACK, D], F32, name="sq")
         log_den = keep.tile([P, PACK, D], F32, name="log_den")
         for t in range(PACK):
-            nc.vector.tensor_tensor(out=soft[:, t, :], in0=log_a[:, t, :], in1=a_bf[:, t, :], op=ALU.max)
+            nc.vector.scalar_tensor_tensor(
+                out=soft[:, t, :], in0=log_a[:, t, :], scalar=LOG_CAP, in1=a_bf[:, t, :], op0=ALU.min, op1=ALU.max
+            )
         for t in range(PACK):
             if t < SQ_ON_SCALAR:
                 nc.scalar.activation(out=sq[:, t, :], in_=soft[:, t, :], func=ACT.Square)
@@ -330,7 +346,7 @@ def tile_laplacepoleresidueoperator_w4_kernel(
                 nc.vector.tensor_tensor(out=sq[:, t, :], in0=soft[:, t, :], in1=soft[:, t, :], op=ALU.mult)
         for t in range(PACK):
             nc.scalar.activation(out=log_den[:, t, :], in_=sq[:, t, :], func=ACT.Ln, bias=w_sq[:, t : t + 1])
-        widen(1, True)
+        widen(1, True, range(EARLY_PLANES, PASSES * PACK))
         interleave(0, True)
         interleave(1, True)
         quantize_v(0)
@@ -353,10 +369,8 @@ def tile_laplacepoleresidueoperator_w4_kernel(
         w_rows = keep.tile([P, 2, M], BF16, name="w_rows")
         for z in range(2):
             nc.scalar.copy(out=as_order(w_rows[:, z, :], z), in_=in_order(w_acc[:, z, :, :], z))
-        make_recip(1)
         widen(2, False)
-        interleave(2, False)
-        widen(3, False)
+        make_recip(1)
 
         count = len(TILES)
         for z in (1, 0):
@@ -364,10 +378,12 @@ def tile_laplacepoleresidueoperator_w4_kernel(
             make_coef_omega(0, z)
         encode(1)
         make_coef_soft(0, 1)
-        product(0, 1, 1)
         make_coef_soft(0, 0)
+        product(0, 1, 1)
         turn_inputs(1)
-        keep_warm(5, 4)
+        interleave_on_tensor(2, 4)
+        keep_warm(5, 2)
+        widen(3, False)
         product(0, 1, 0)
         add_terms(0, 1, nc.gpsimd)
         product(0, 0, 0)
@@ -396,19 +412,19 @@ def tile_laplacepoleresidueoperator_w4_kernel(
                     make_coef_soft(1, 0)
                 product(j, 0, 0)
                 product(j, 0, 1)
-            if j == 2:
-                keep_warm(6, 4)
             turn_real(j - 1)
             turn_pairs(j - 1, 1, nc.vector.tensor_copy if j == count else nc.scalar.copy)
-            if j in (2, 3):
+            if j == 2:
+                interleave_on_tensor(4, 6)
+            if j == 3:
                 keep_warm(6, 2)
             if j + 1 < count:
                 encode(j + 1)
-            if j < AHEAD_FROM:
-                interleave(j + 2, False)
+            if j == 1:
+                interleave_on_tensor(3, 6)
             if AHEAD_FROM - 1 <= j < count - 3:
                 interleave(j + 3, False)
             if j >= 2:
-                decode(j - 2, (6, 7), (nc.scalar.copy,))
+                decode(j - 2, (6, 7, 0, 1) if j >= FINE_FROM else (6, 7), (nc.scalar.copy,))
         quantize_z(count - 1)
-        decode(count - 1, (0, 1, 2, 3), (nc.vector.tensor_copy, nc.scalar.copy))
+        decode(count - 1, (2, 3, 4, 5), (nc.vector.tensor_copy, nc.scalar.copy))

@@ -21,15 +21,26 @@ ACT = mybir.ActivationFunctionType
 P = 128
 PACK = 4
 PASSES = 2
+PLANES = PASSES * PACK
+RUN = 4
 HALVES = D // P
+REAL, IMAG = 0, 1
+
 TILES = [(b, dh) for dh in range(HALVES) for b in range(B)]
-AHEAD_FROM = 3
-REAL_AS_PAIRS = (4, 5, 6)
-OMEGA_ENGINE = lambda nc, dh, z: nc.gpsimd
+COUNT = len(TILES)
+
+C_BANKS = 4
+Z_BANK = 4
+OUT_BANKS = (6, 7)
+OMEGA_BANK = 3
+LATE_OUT_BANKS = ((6, 7, 0, 1), (2, 3, 4, 5))
+
 LOG_CAP = 40.0
-SQ_ON_SCALAR = 2
-FINE_FROM = 7
+SQUARES_ON_SCALAR = 2
 EARLY_PLANES = 2
+REAL_AS_PAIRS = range(B, COUNT - 1)
+AHEAD_FROM = 3
+WARM_LONG, WARM_SHORT = 4, 2
 
 
 def tile_laplacepoleresidueoperator_w4_kernel(
@@ -46,11 +57,11 @@ def tile_laplacepoleresidueoperator_w4_kernel(
             return psum.tile(shape, dtype, name=name, tag="bank%d" % index)
 
         a_bf = keep.tile([P, PACK, D], BF16, name="a_bf")
-        for u in range(2):
-            nc.sync.dma_start(out=a_bf[:, 2 * u : 2 * u + 2, :], in_=alpha.rearrange("(p t) d -> p t d", t=PACK)[:, 2 * u : 2 * u + 2, :])
+        slot_pairs = [slice(2 * u, 2 * u + 2) for u in range(2)]
+        for pair in slot_pairs:
+            nc.sync.dma_start(out=a_bf[:, pair, :], in_=alpha.rearrange("(p t) d -> p t d", t=PACK)[:, pair, :])
         vs = keep.tile([P, PASSES, PACK], F32, name="vs")
         nc.sync.dma_start(out=vs[:], in_=v_scale.rearrange("o (g p t) x -> p (o g) (t x)", p=P, t=PACK))
-
 
         v_raw = []
 
@@ -86,7 +97,7 @@ def tile_laplacepoleresidueoperator_w4_kernel(
         nc.sync.dma_start(out=w_bf[:], in_=omega.rearrange("(p t) -> p t", t=PACK))
         load_v(1)
         beta_bf = keep.tile([P, 2, PACK, D], BF16, name="beta_bf")
-        nc.sync.dma_start(out=beta_bf[:], in_=beta.rearrange("(h p t) d -> p h t d", p=P, t=PACK))
+        nc.sync.dma_start(out=beta_bf[:], in_=beta.rearrange("(z p t) d -> p z t d", p=P, t=PACK))
         enc_w = load_words(enc_words, "enc_w")
         load_scales(enc_s, enc_scales)
         load_scales(dec_s, dec_scales)
@@ -96,46 +107,25 @@ def tile_laplacepoleresidueoperator_w4_kernel(
 
         wide = {}
 
-        def widen(b, on_vector, planes=range(PASSES * PACK)):
+        def widen(b, on_vector, planes):
             if b not in wide:
                 wide[b] = keep.tile([P, PASSES, PACK, D], BF16, name="wide%d" % b)
-            tile = wide[b]
             for plane in planes:
-                for g, t in [divmod(plane, PACK)]:
-                    src = v_raw[b][:, g, t * D : (t + 1) * D].bitcast(FP8)
-                    if on_vector:
-                        nc.vector.tensor_scalar(
-                            out=tile[:, g, t, :], in0=src, scalar1=vs[:, g, t : t + 1], scalar2=None, op0=ALU.mult
-                        )
-                    else:
-                        nc.scalar.activation(out=tile[:, g, t, :], in_=src, func=ACT.Copy, scale=vs[:, g, t : t + 1])
+                g, t = divmod(plane, PACK)
+                src = v_raw[b][:, g, t * D : (t + 1) * D].bitcast(FP8)
+                scale = vs[:, g, t : t + 1]
+                if on_vector:
+                    nc.vector.tensor_scalar(out=wide[b][:, g, t, :], in0=src, scalar1=scale, scalar2=None, op0=ALU.mult)
+                else:
+                    nc.scalar.activation(out=wide[b][:, g, t, :], in_=src, func=ACT.Copy, scale=scale)
 
         grouped = {}
 
-        def interleave(j, on_vector):
+        def interleave(j, copy):
             b, dh = TILES[j]
             tile = work.tile([P, PASSES, P, PACK], BF16, name="v_grouped", bufs=3, align_bytes=64)
-            dst = tile[:].rearrange("p g (c i) t -> p g c t i", i=4)
-            src = wide[b][:, :, :, dh * P : (dh + 1) * P].rearrange("p g t (c i) -> p g c t i", i=4)
-            if on_vector:
-                nc.vector.tensor_copy(out=dst, in_=src)
-            else:
-                nc.scalar.copy(out=dst, in_=src)
-            grouped[j] = tile
-
-        def interleave_on_tensor(j, index):
-            b, dh = TILES[j]
-            tile = work.tile([P, PASSES, P, PACK], BF16, name="v_grouped", bufs=3, align_bytes=64)
-            acc = bank(index, [P, PASSES, P, PACK], BF16, "v_acc")
-            for g in range(PASSES):
-                nc.tensor.matmul(
-                    out=acc[:, g, :, :],
-                    lhsT=ident_bf[:],
-                    rhs=wide[b][:, g, :, dh * P : (dh + 1) * P].rearrange("p t c -> p c t"),
-                    start=True,
-                    stop=True,
-                )
-            nc.scalar.copy(out=tile[:], in_=acc[:])
+            src = wide[b][:, :, :, dh * P : (dh + 1) * P].rearrange("p g t (c r) -> p g c t r", r=RUN)
+            copy(out=tile[:].rearrange("p g (c r) t -> p g c t r", r=RUN), in_=src)
             grouped[j] = tile
 
         def quantize(src, name, bufs):
@@ -153,12 +143,12 @@ def tile_laplacepoleresidueoperator_w4_kernel(
         def quantize_v(j):
             v_mx[j] = quantize(grouped[j], "v", 3)
 
-        c_banks = {}
+        c_acc = {}
 
         def encode(j):
             codes, scales = v_mx[j]
-            for h in range(2):
-                acc = bank((2 * j + h) % 4, [P, M], F32, "c_acc")
+            for h in (REAL, IMAG):
+                acc = bank((2 * j + h) % C_BANKS, [P, M], F32, "c_acc")
                 for g in range(PASSES):
                     nc.tensor.matmul_mx(
                         out=acc[:],
@@ -169,64 +159,71 @@ def tile_laplacepoleresidueoperator_w4_kernel(
                         start=(g == 0),
                         stop=(g == PASSES - 1),
                     )
-                c_banks[(j, h)] = acc
+                c_acc[(j, h)] = acc
 
+        def stored(ap, as_pairs):
+            if as_pairs:
+                return ap.rearrange("d (u p e) -> d u p e", u=2, e=2)
+            return ap.rearrange("d (t p) -> d t p", t=PACK)
+
+        def walked(ap, as_pairs):
+            if as_pairs:
+                return ap.rearrange("d (u e) p -> d u p e", u=2)
+            return ap
+
+        coef = {}
         terms = {}
 
         def product(j, z, h):
-            dh = TILES[j][1]
             tile = work.tile([P, M], F32, name="term%d%d" % (z, h))
-            factor = coef[(dh, z, h)][:]
-            if z == 0 and j not in REAL_AS_PAIRS:
-                src = c_banks[(j, h)][:].rearrange("d (p t) -> d t p", t=PACK)
-                dst = tile[:].rearrange("d (t p) -> d t p", t=PACK)
-                factor = factor.rearrange("d (t p) -> d t p", t=PACK)
+            as_pairs = z == IMAG or j in REAL_AS_PAIRS
+            if as_pairs:
+                src = c_acc[(j, h)][:].rearrange("d (p u e) -> d u p e", u=2, e=2)
             else:
-                src = c_banks[(j, h)][:].rearrange("d (p u e) -> d u p e", u=2, e=2)
-                dst = tile[:].rearrange("d (u p e) -> d u p e", u=2, e=2)
-                if z == 0:
-                    factor = factor.rearrange("d (u e p) -> d u p e", u=2, e=2)
-                else:
-                    factor = factor.rearrange("d (u p e) -> d u p e", u=2, e=2)
-            nc.vector.tensor_tensor(out=dst, in0=src, in1=factor, op=ALU.mult)
+                src = c_acc[(j, h)][:].rearrange("d (p t) -> d t p", t=PACK)
+            factor = stored(coef[(TILES[j][1], z, h)][:], z == IMAG)
+            if z == REAL:
+                factor = walked(factor, as_pairs)
+            nc.vector.tensor_tensor(out=stored(tile[:], as_pairs), in0=src, in1=factor, op=ALU.mult)
             terms[(j, z, h)] = tile
 
         z_sum = {}
 
         def add_terms(j, z, engine):
             tile = work.tile([P, M], BF16, name="z_sum%d" % z)
-            engine.tensor_tensor(out=tile[:], in0=terms[(j, z, 0)][:], in1=terms[(j, z, 1)][:], op=ALU.add)
+            engine.tensor_tensor(out=tile[:], in0=terms[(j, z, REAL)][:], in1=terms[(j, z, IMAG)][:], op=ALU.add)
             z_sum[(j, z)] = tile
 
         z_bf = {}
 
         def turn_and_add(j):
-            acc = bank(4, [P, PACK, P], F32, "z_acc")
+            acc = bank(Z_BANK + REAL, [P, PACK, P], F32, "z_acc")
             for t in range(PACK):
-                for h in range(2):
+                for h in (REAL, IMAG):
                     nc.tensor.matmul(
                         out=acc[:, t, :],
-                        lhsT=terms[(j, 0, h)][:, t * P : (t + 1) * P],
+                        lhsT=terms[(j, REAL, h)][:, t * P : (t + 1) * P],
                         rhs=ident[:],
                         is_transpose=True,
-                        start=(h == 0),
-                        stop=(h == 1),
+                        start=(h == REAL),
+                        stop=(h == IMAG),
                     )
-            nc.scalar.copy(out=z_bf[j][:, 0, :, :], in_=acc[:].rearrange("p t d -> p d t"))
+            nc.scalar.copy(out=z_bf[j][:, REAL, :, :], in_=acc[:].rearrange("p t d -> p d t"))
 
         def turn_pairs(j, z, copy):
-            pairs = bank(4 + z, [P, 2, P], F32, "z_pairs")
+            acc = bank(Z_BANK + z, [P, 2, P], F32, "z_pairs")
             words = z_sum[(j, z)][:].bitcast(F32)
             for u in range(2):
-                nc.tensor.transpose(pairs[:, u, :], words[:, u * P : (u + 1) * P], ident[:])
-            copy(out=z_bf[j][:, z, :, :].bitcast(F32), in_=pairs[:].rearrange("p u d -> p d u"))
+                nc.tensor.transpose(acc[:, u, :], words[:, u * P : (u + 1) * P], ident[:])
+            copy(out=z_bf[j][:, z, :, :].bitcast(F32), in_=acc[:].rearrange("p u d -> p d u"))
 
-        def turn_real(j):
+        def turn_z(j, copy_imag):
             z_bf[j] = work.tile([P, 2, P, PACK], BF16, name="z_bf", align_bytes=64)
             if j in REAL_AS_PAIRS:
-                turn_pairs(j, 0, nc.scalar.copy)
+                turn_pairs(j, REAL, nc.scalar.copy)
             else:
                 turn_and_add(j)
+            turn_pairs(j, IMAG, copy_imag)
 
         z_mx = {}
 
@@ -256,46 +253,42 @@ def tile_laplacepoleresidueoperator_w4_kernel(
                 rows = out[b, per_bank * o * P : per_bank * (o + 1) * P, dh * P : (dh + 1) * P]
                 nc.sync.dma_start(out=rows.rearrange("(i p) d -> p i d", p=P), in_=result[:])
 
-        def turn(slices, index, name):
+        def keep_warm(index, repeats):
+            acc = bank(index, [P, M], F32, "warm")
+            moving = beta_bf[:, REAL, slot_pairs[0], :].rearrange("p t d -> p (t d)")
+            for repeat in range(repeats):
+                nc.tensor.matmul(out=acc[:], lhsT=ident_bf[:], rhs=moving, start=True, stop=True)
+
+        def turn_f32(src, dh, index, name):
             acc = bank(index, [P, PACK, P], F32, name)
             for t in range(PACK):
-                nc.tensor.transpose(acc[:, t, :], slices[t], ident[:])
+                nc.tensor.transpose(acc[:, t, :], src[:, t, dh * P : (dh + 1) * P], ident[:])
             return acc
 
-        def keep_warm(index, passes):
-            acc = bank(index, [P, M], F32, "warm")
-            for i in range(passes):
-                nc.tensor.matmul(out=acc[:], lhsT=ident_bf[:], rhs=beta_bf[:, 0, 0:2, :].rearrange("p t d -> p (t d)"), start=True, stop=True)
-
-        turned = {}
+        beta_t = {}
+        soft_t = {}
 
         def turn_inputs(dh):
-            cols = slice(dh * P, (dh + 1) * P)
-            acc = bank(6, [P, 2, PACK, P], BF16, "beta_t")
-            for z in range(2):
+            beta_t[dh] = bank(OUT_BANKS[0], [P, 2, PACK, P], BF16, "beta_t")
+            for z in (REAL, IMAG):
                 for t in range(PACK):
-                    nc.tensor.transpose(acc[:, z, t, :], beta_bf[:, z, t, cols], ident_bf[:])
-            turned[dh] = (acc, turn([soft[:, t, cols] for t in range(PACK)], 7, "soft_t"))
+                    nc.tensor.transpose(beta_t[dh][:, z, t, :], beta_bf[:, z, t, dh * P : (dh + 1) * P], ident_bf[:])
+            soft_t[dh] = turn_f32(soft, dh, OUT_BANKS[1], "soft_t")
 
-        def in_order(ap, z):
-            if z == 0:
-                return ap
-            return ap.rearrange("d (u e) p -> d u p e", u=2)
+        recip = {}
 
-        def as_order(ap, z):
-            if z == 0:
-                return ap.rearrange("d (t p) -> d t p", t=PACK)
-            return ap.rearrange("d (u p e) -> d u p e", u=2, e=2)
+        def make_recip(dh):
+            recip[dh] = keep.tile([P, PACK, P], F32, name="recip%d" % dh)
+            nc.scalar.activation(out=recip[dh][:], in_=log_den_t[dh][:], func=ACT.Exp, scale=-1.0)
 
         gain = {}
-        coef = {}
 
         def make_gain(dh, z):
             tile = keep.tile([P, M], F32, name="gain%d%d" % (dh, z))
             nc.vector.tensor_tensor(
-                out=as_order(tile[:], z),
-                in0=in_order(turned[dh][0][:, z, :, :], z),
-                in1=in_order(recip[dh][:], z),
+                out=stored(tile[:], z == IMAG),
+                in0=walked(beta_t[dh][:, z, :, :], z == IMAG),
+                in1=walked(recip[dh][:], z == IMAG),
                 op=ALU.mult,
             )
             gain[(dh, z)] = tile
@@ -303,29 +296,31 @@ def tile_laplacepoleresidueoperator_w4_kernel(
         def make_coef_soft(dh, z):
             tile = keep.tile([P, M], F32, name="coef%d%d%d" % (dh, z, z))
             nc.vector.tensor_tensor(
-                out=as_order(tile[:], z), in0=in_order(turned[dh][1][:], z), in1=as_order(gain[(dh, z)][:], z), op=ALU.mult
+                out=stored(tile[:], z == IMAG),
+                in0=walked(soft_t[dh][:], z == IMAG),
+                in1=stored(gain[(dh, z)][:], z == IMAG),
+                op=ALU.mult,
             )
             coef[(dh, z, z)] = tile
 
         def make_coef_omega(dh, z):
             tile = keep.tile([P, M], F32, name="coef%d%d%d" % (dh, z, 1 - z))
-            OMEGA_ENGINE(nc, dh, z).tensor_tensor(out=tile[:], in0=gain[(dh, z)][:], in1=w_rows[:, z, :], op=ALU.mult)
+            nc.gpsimd.tensor_tensor(out=tile[:], in0=gain[(dh, z)][:], in1=w_rows[:, z, :], op=ALU.mult)
             coef[(dh, z, 1 - z)] = tile
 
         exp_a = keep.tile([P, PACK, D], F32, name="exp_a")
-        for u in range(2):
-            nc.scalar.activation(out=exp_a[:, 2 * u : 2 * u + 2, :], in_=a_bf[:, 2 * u : 2 * u + 2, :], func=ACT.Exp)
-        widen(0, True)
+        for pair in slot_pairs:
+            nc.scalar.activation(out=exp_a[:, pair, :], in_=a_bf[:, pair, :], func=ACT.Exp)
+        widen(0, True, range(PLANES))
         w_sq = keep.tile([P, PACK], F32, name="w_sq")
         nc.vector.tensor_tensor(out=w_sq[:], in0=w_bf[:], in1=w_bf[:], op=ALU.mult)
         w_neg = keep.tile([P, PACK], BF16, name="w_neg")
         nc.vector.tensor_scalar(out=w_neg[:], in0=w_bf[:], scalar1=-1.0, scalar2=None, op0=ALU.mult)
-        w_acc = bank(3, [P, 2, PACK, P], BF16, "w_acc")
-        for z, col in enumerate((w_bf, w_neg)):
+        w_acc = bank(OMEGA_BANK, [P, 2, PACK, P], BF16, "w_acc")
+        for z, signed in ((REAL, w_bf), (IMAG, w_neg)):
             for t in range(PACK):
-                nc.tensor.matmul(
-                    out=w_acc[:, z, t, :], lhsT=col[:, t : t + 1].to_broadcast([P, P]), rhs=ident_bf[:], start=True, stop=True
-                )
+                column = signed[:, t : t + 1].to_broadcast([P, P])
+                nc.tensor.matmul(out=w_acc[:, z, t, :], lhsT=column, rhs=ident_bf[:], start=True, stop=True)
 
         log_a = keep.tile([P, PACK, D], F32, name="log_a")
         for t in range(PACK):
@@ -333,98 +328,88 @@ def tile_laplacepoleresidueoperator_w4_kernel(
 
         widen(1, True, range(EARLY_PLANES))
         soft = keep.tile([P, PACK, D], F32, name="soft")
-        sq = keep.tile([P, PACK, D], F32, name="sq")
+        soft_sq = keep.tile([P, PACK, D], F32, name="soft_sq")
         log_den = keep.tile([P, PACK, D], F32, name="log_den")
         for t in range(PACK):
             nc.vector.scalar_tensor_tensor(
                 out=soft[:, t, :], in0=log_a[:, t, :], scalar=LOG_CAP, in1=a_bf[:, t, :], op0=ALU.min, op1=ALU.max
             )
         for t in range(PACK):
-            if t < SQ_ON_SCALAR:
-                nc.scalar.activation(out=sq[:, t, :], in_=soft[:, t, :], func=ACT.Square)
+            if t < SQUARES_ON_SCALAR:
+                nc.scalar.activation(out=soft_sq[:, t, :], in_=soft[:, t, :], func=ACT.Square)
             else:
-                nc.vector.tensor_tensor(out=sq[:, t, :], in0=soft[:, t, :], in1=soft[:, t, :], op=ALU.mult)
+                nc.vector.tensor_tensor(out=soft_sq[:, t, :], in0=soft[:, t, :], in1=soft[:, t, :], op=ALU.mult)
         for t in range(PACK):
-            nc.scalar.activation(out=log_den[:, t, :], in_=sq[:, t, :], func=ACT.Ln, bias=w_sq[:, t : t + 1])
-        widen(1, True, range(EARLY_PLANES, PASSES * PACK))
-        interleave(0, True)
-        interleave(1, True)
+            nc.scalar.activation(out=log_den[:, t, :], in_=soft_sq[:, t, :], func=ACT.Ln, bias=w_sq[:, t : t + 1])
+        widen(1, True, range(EARLY_PLANES, PLANES))
+        interleave(0, nc.vector.tensor_copy)
+        interleave(1, nc.vector.tensor_copy)
         quantize_v(0)
         quantize_v(1)
         turn_inputs(0)
-        log_den_t = []
-        for dh in range(HALVES):
-            log_den_t.append(turn([log_den[:, t, dh * P : (dh + 1) * P] for t in range(PACK)], 4 + dh, "log_den_t"))
-        keep_warm(2, 4)
+        log_den_t = [turn_f32(log_den, dh, Z_BANK + dh, "log_den_t") for dh in range(HALVES)]
+        keep_warm(OMEGA_BANK - 1, WARM_LONG)
         encode(0)
-
-        recip = {}
-
-        def make_recip(dh):
-            tile = keep.tile([P, PACK, P], F32, name="recip%d" % dh)
-            nc.scalar.activation(out=tile[:], in_=log_den_t[dh][:], func=ACT.Exp, scale=-1.0)
-            recip[dh] = tile
 
         make_recip(0)
         w_rows = keep.tile([P, 2, M], BF16, name="w_rows")
-        for z in range(2):
-            nc.scalar.copy(out=as_order(w_rows[:, z, :], z), in_=in_order(w_acc[:, z, :, :], z))
-        widen(2, False)
+        for z in (REAL, IMAG):
+            nc.scalar.copy(out=stored(w_rows[:, z, :], z == IMAG), in_=walked(w_acc[:, z, :, :], z == IMAG))
         make_recip(1)
+        widen(2, False, range(PLANES))
+        interleave(2, nc.scalar.copy)
+        widen(3, False, range(PLANES))
 
-        count = len(TILES)
-        for z in (1, 0):
+        for z in (IMAG, REAL):
             make_gain(0, z)
             make_coef_omega(0, z)
         encode(1)
-        make_coef_soft(0, 1)
-        make_coef_soft(0, 0)
-        product(0, 1, 1)
+        make_coef_soft(0, IMAG)
+        make_coef_soft(0, REAL)
+        product(0, IMAG, IMAG)
         turn_inputs(1)
-        interleave_on_tensor(2, 4)
-        keep_warm(5, 2)
-        widen(3, False)
-        product(0, 1, 0)
-        add_terms(0, 1, nc.gpsimd)
-        product(0, 0, 0)
-        product(0, 0, 1)
-        for j in range(1, count + 1):
-            if j < count:
-                product(j, 1, 0)
+        keep_warm(Z_BANK + IMAG, WARM_LONG)
+        product(0, IMAG, REAL)
+        add_terms(0, IMAG, nc.gpsimd)
+        product(0, REAL, REAL)
+        product(0, REAL, IMAG)
+
+        for j in range(1, COUNT + 1):
+            if j < COUNT:
+                product(j, IMAG, REAL)
             if j - 1 in REAL_AS_PAIRS:
-                add_terms(j - 1, 0, nc.vector)
+                add_terms(j - 1, REAL, nc.vector)
             if j >= 2:
                 quantize_z(j - 2)
             if j <= AHEAD_FROM:
                 quantize_v(j + 1)
-            if AHEAD_FROM <= j < count - 2:
+            if AHEAD_FROM <= j < COUNT - 2:
                 quantize_v(j + 2)
-            if j < count:
-                product(j, 1, 1)
-                add_terms(j, 1, nc.gpsimd)
+            if j < COUNT:
+                product(j, IMAG, IMAG)
+                add_terms(j, IMAG, nc.gpsimd)
                 if j == 1:
-                    make_gain(1, 1)
-                    make_coef_omega(1, 1)
-                    make_gain(1, 0)
+                    make_gain(1, IMAG)
+                    make_coef_omega(1, IMAG)
+                    make_gain(1, REAL)
                 if j == 2:
-                    make_coef_omega(1, 0)
-                    make_coef_soft(1, 1)
-                    make_coef_soft(1, 0)
-                product(j, 0, 0)
-                product(j, 0, 1)
-            turn_real(j - 1)
-            turn_pairs(j - 1, 1, nc.vector.tensor_copy if j == count else nc.scalar.copy)
+                    make_coef_omega(1, REAL)
+                    make_coef_soft(1, IMAG)
+                    make_coef_soft(1, REAL)
+                product(j, REAL, REAL)
+                product(j, REAL, IMAG)
             if j == 2:
-                interleave_on_tensor(4, 6)
-            if j == 3:
-                keep_warm(6, 2)
-            if j + 1 < count:
+                keep_warm(OUT_BANKS[0], WARM_LONG)
+            turn_z(j - 1, nc.vector.tensor_copy if j == COUNT else nc.scalar.copy)
+            if j in (2, 3):
+                keep_warm(OUT_BANKS[0], WARM_SHORT)
+            if j + 1 < COUNT:
                 encode(j + 1)
-            if j == 1:
-                interleave_on_tensor(3, 6)
-            if AHEAD_FROM - 1 <= j < count - 3:
-                interleave(j + 3, False)
+            if j < AHEAD_FROM:
+                interleave(j + 2, nc.scalar.copy)
+            if AHEAD_FROM - 1 <= j < COUNT - 3:
+                interleave(j + 3, nc.scalar.copy)
             if j >= 2:
-                decode(j - 2, (6, 7, 0, 1) if j >= FINE_FROM else (6, 7), (nc.scalar.copy,))
-        quantize_z(count - 1)
-        decode(count - 1, (2, 3, 4, 5), (nc.vector.tensor_copy, nc.scalar.copy))
+                decode(j - 2, LATE_OUT_BANKS[0] if j == COUNT else OUT_BANKS, (nc.scalar.copy,))
+        quantize_z(COUNT - 1)
+        decode(COUNT - 1, LATE_OUT_BANKS[1], (nc.vector.tensor_copy, nc.scalar.copy))

from contextlib import ExitStack

import concourse.mybir as mybir
from concourse.masks import make_identity

B, N, D, M = 4, 1024, 256, 512
M2 = 2 * M
FLOPS = 2 * 2 * B * N * M2 * D

F32 = mybir.dt.float32
BF16 = mybir.dt.bfloat16
I32 = mybir.dt.int32
U32 = mybir.dt.uint32
U8 = mybir.dt.uint8
FP8 = mybir.dt.float8_e4m3fn
FP8X4 = mybir.dt.float8_e4m3fn_x4
FP4X4 = mybir.dt.float4_e2m1fn_x4
ALU = mybir.AluOpType
ACT = mybir.ActivationFunctionType

P = 128
PACK = 4
PASSES = 2
PLANES = PASSES * PACK
RUN = 4
HALVES = D // P
REAL, IMAG = 0, 1

TILES = [(b, dh) for dh in range(HALVES) for b in range(B)]
COUNT = len(TILES)

C_BANKS = 4
Z_BANK = 4
OUT_BANKS = (6, 7)
OMEGA_BANK = 3
LATE_OUT_BANKS = ((6, 7, 0, 1), (2, 3, 4, 5))

LOG_CAP = 40.0
SQUARES_ON_SCALAR = 2
EARLY_PLANES = 2
REAL_AS_PAIRS = range(B, COUNT - 1)
AHEAD_FROM = 3
WARM_LONG, WARM_SHORT = 4, 2


def tile_laplacepoleresidueoperator_w4_kernel(
    tc, v_bytes, v_scale, enc_words, enc_scales, dec_words, dec_scales, alpha, omega, beta, out
):
    nc = tc.nc
    with ExitStack() as ctx:
        keep = ctx.enter_context(tc.tile_pool(name="keep", bufs=1))
        work = ctx.enter_context(tc.tile_pool(name="work", bufs=2))
        psum = ctx.enter_context(tc.psum_pool(name="psum", bufs=1))
        ctx.enter_context(tc.manual_schedule())

        def bank(index, shape, dtype, name):
            return psum.tile(shape, dtype, name=name, tag="bank%d" % index)

        a_bf = keep.tile([P, PACK, D], BF16, name="a_bf")
        slot_pairs = [slice(2 * u, 2 * u + 2) for u in range(2)]
        for pair in slot_pairs:
            nc.sync.dma_start(out=a_bf[:, pair, :], in_=alpha.rearrange("(p t) d -> p t d", t=PACK)[:, pair, :])
        vs = keep.tile([P, PASSES, PACK], F32, name="vs")
        nc.sync.dma_start(out=vs[:], in_=v_scale.rearrange("o (g p t) x -> p (o g) (t x)", p=P, t=PACK))

        v_raw = []

        def load_v(b):
            raw = keep.tile([P, PASSES, PACK * D], U8, name="v_raw%d" % b)
            nc.sync.dma_start(out=raw[:], in_=v_bytes[b].rearrange("(g p t) d -> p g (t d)", p=P, t=PACK))
            v_raw.append(raw)

        def load_words(words, name):
            tile = keep.tile([P, PASSES, 2 * N], U8, name=name, align_bytes=64)
            nc.sync.dma_start(out=tile[:].bitcast(I32), in_=words.rearrange("g p n -> p g n").bitcast(I32))
            return tile

        def load_scales(tile, scales):
            for q in range(4):
                nc.sync.dma_start(
                    out=tile[32 * q : 32 * q + 4, :, :].bitcast(I32),
                    in_=scales[:, 4 * q : 4 * q + 4, :].rearrange("g r n -> r g n").bitcast(I32),
                )

        enc_s = keep.tile([P, PASSES, M2], U8, name="enc_s", align_bytes=64)
        dec_s = keep.tile([P, PASSES, N], U8, name="dec_s", align_bytes=64)
        ident = keep.tile([P, P], F32, name="ident")
        nc.vector.memset(ident[:], 0.0)
        make_identity(nc, ident[:], nomemset=True)
        nc.vector.memset(enc_s[:].bitcast(I32), 0)
        nc.vector.memset(dec_s[:].bitcast(I32), 0)
        ident_bf = keep.tile([P, P], BF16, name="ident_bf")
        nc.scalar.copy(out=ident_bf[:], in_=ident[:])

        load_v(0)
        w_bf = keep.tile([P, PACK], BF16, name="w_bf")
        nc.sync.dma_start(out=w_bf[:], in_=omega.rearrange("(p t) -> p t", t=PACK))
        load_v(1)
        beta_bf = keep.tile([P, 2, PACK, D], BF16, name="beta_bf")
        nc.sync.dma_start(out=beta_bf[:], in_=beta.rearrange("(z p t) d -> p z t d", p=P, t=PACK))
        enc_w = load_words(enc_words, "enc_w")
        load_scales(enc_s, enc_scales)
        load_scales(dec_s, dec_scales)
        load_v(2)
        load_v(3)
        dec_w = load_words(dec_words, "dec_w")

        wide = {}

        def widen(b, on_vector, planes):
            if b not in wide:
                wide[b] = keep.tile([P, PASSES, PACK, D], BF16, name="wide%d" % b)
            for plane in planes:
                g, t = divmod(plane, PACK)
                src = v_raw[b][:, g, t * D : (t + 1) * D].bitcast(FP8)
                scale = vs[:, g, t : t + 1]
                if on_vector:
                    nc.vector.tensor_scalar(out=wide[b][:, g, t, :], in0=src, scalar1=scale, scalar2=None, op0=ALU.mult)
                else:
                    nc.scalar.activation(out=wide[b][:, g, t, :], in_=src, func=ACT.Copy, scale=scale)

        grouped = {}

        def interleave(j, copy):
            b, dh = TILES[j]
            tile = work.tile([P, PASSES, P, PACK], BF16, name="v_grouped", bufs=3, align_bytes=64)
            src = wide[b][:, :, :, dh * P : (dh + 1) * P].rearrange("p g t (c r) -> p g c t r", r=RUN)
            copy(out=tile[:].rearrange("p g (c r) t -> p g c t r", r=RUN), in_=src)
            grouped[j] = tile

        def quantize(src, name, bufs):
            codes = work.tile([P, PASSES, P], U32, name=name + "_codes", bufs=bufs, align_bytes=64)
            scales = work.tile([P, PASSES, P], U8, name=name + "_scales", bufs=bufs, align_bytes=64)
            nc.vector.quantize_mx(
                out=codes[:].rearrange("p g c -> p (g c)").bitcast(FP8X4),
                scales=scales[:].rearrange("p g c -> p (g c)"),
                in_=src[:].rearrange("p g c t -> p (g c t)"),
            )
            return codes, scales

        v_mx = {}

        def quantize_v(j):
            v_mx[j] = quantize(grouped[j], "v", 3)

        c_acc = {}

        def encode(j):
            codes, scales = v_mx[j]
            for h in (REAL, IMAG):
                acc = bank((2 * j + h) % C_BANKS, [P, M], F32, "c_acc")
                for g in range(PASSES):
                    nc.tensor.matmul_mx(
                        out=acc[:],
                        lhsT=codes[:, g, :].bitcast(FP8X4),
                        lhsT_scale=scales[:, g, :],
                        rhs=enc_w[:, g, 2 * M * h : 2 * M * (h + 1)].bitcast(FP4X4),
                        rhs_scale=enc_s[:, g, M * h : M * (h + 1)],
                        start=(g == 0),
                        stop=(g == PASSES - 1),
                    )
                c_acc[(j, h)] = acc

        def stored(ap, as_pairs):
            if as_pairs:
                return ap.rearrange("d (u p e) -> d u p e", u=2, e=2)
            return ap.rearrange("d (t p) -> d t p", t=PACK)

        def walked(ap, as_pairs):
            if as_pairs:
                return ap.rearrange("d (u e) p -> d u p e", u=2)
            return ap

        coef = {}
        terms = {}

        def product(j, z, h):
            tile = work.tile([P, M], F32, name="term%d%d" % (z, h))
            as_pairs = z == IMAG or j in REAL_AS_PAIRS
            if as_pairs:
                src = c_acc[(j, h)][:].rearrange("d (p u e) -> d u p e", u=2, e=2)
            else:
                src = c_acc[(j, h)][:].rearrange("d (p t) -> d t p", t=PACK)
            factor = stored(coef[(TILES[j][1], z, h)][:], z == IMAG)
            if z == REAL:
                factor = walked(factor, as_pairs)
            nc.vector.tensor_tensor(out=stored(tile[:], as_pairs), in0=src, in1=factor, op=ALU.mult)
            terms[(j, z, h)] = tile

        z_sum = {}

        def add_terms(j, z, engine):
            tile = work.tile([P, M], BF16, name="z_sum%d" % z)
            engine.tensor_tensor(out=tile[:], in0=terms[(j, z, REAL)][:], in1=terms[(j, z, IMAG)][:], op=ALU.add)
            z_sum[(j, z)] = tile

        z_bf = {}

        def turn_and_add(j):
            acc = bank(Z_BANK + REAL, [P, PACK, P], F32, "z_acc")
            for t in range(PACK):
                for h in (REAL, IMAG):
                    nc.tensor.matmul(
                        out=acc[:, t, :],
                        lhsT=terms[(j, REAL, h)][:, t * P : (t + 1) * P],
                        rhs=ident[:],
                        is_transpose=True,
                        start=(h == REAL),
                        stop=(h == IMAG),
                    )
            nc.scalar.copy(out=z_bf[j][:, REAL, :, :], in_=acc[:].rearrange("p t d -> p d t"))

        def turn_pairs(j, z, copy):
            acc = bank(Z_BANK + z, [P, 2, P], F32, "z_pairs")
            words = z_sum[(j, z)][:].bitcast(F32)
            for u in range(2):
                nc.tensor.transpose(acc[:, u, :], words[:, u * P : (u + 1) * P], ident[:])
            copy(out=z_bf[j][:, z, :, :].bitcast(F32), in_=acc[:].rearrange("p u d -> p d u"))

        def turn_z(j, copy_imag):
            z_bf[j] = work.tile([P, 2, P, PACK], BF16, name="z_bf", align_bytes=64)
            if j in REAL_AS_PAIRS:
                turn_pairs(j, REAL, nc.scalar.copy)
            else:
                turn_and_add(j)
            turn_pairs(j, IMAG, copy_imag)

        z_mx = {}

        def quantize_z(j):
            z_mx[j] = quantize(z_bf[j], "z", 2)

        def decode(j, banks, copies):
            b, dh = TILES[j]
            codes, scales = z_mx[j]
            per_bank = N // P // len(banks)
            for o, index in enumerate(banks):
                acc = bank(index, [P, per_bank, P], F32, "o_acc")
                for i in range(per_bank):
                    n0 = (per_bank * o + i) * P
                    for g in range(PASSES):
                        nc.tensor.matmul_mx(
                            out=acc[:, i, :],
                            lhsT=dec_w[:, g, 2 * n0 : 2 * (n0 + P)].bitcast(FP4X4),
                            lhsT_scale=dec_s[:, g, n0 : n0 + P],
                            rhs=codes[:, g, :].bitcast(FP8X4),
                            rhs_scale=scales[:, g, :],
                            start=(g == 0),
                            stop=(g == PASSES - 1),
                        )
                result = work.tile([P, per_bank, P], F32, name="result", bufs=8)
                copies[o % len(copies)](out=result[:], in_=acc[:])
                rows = out[b, per_bank * o * P : per_bank * (o + 1) * P, dh * P : (dh + 1) * P]
                nc.sync.dma_start(out=rows.rearrange("(i p) d -> p i d", p=P), in_=result[:])

        def keep_warm(index, repeats):
            acc = bank(index, [P, M], F32, "warm")
            moving = beta_bf[:, REAL, slot_pairs[0], :].rearrange("p t d -> p (t d)")
            for repeat in range(repeats):
                nc.tensor.matmul(out=acc[:], lhsT=ident_bf[:], rhs=moving, start=True, stop=True)

        def turn_f32(src, dh, index, name):
            acc = bank(index, [P, PACK, P], F32, name)
            for t in range(PACK):
                nc.tensor.transpose(acc[:, t, :], src[:, t, dh * P : (dh + 1) * P], ident[:])
            return acc

        beta_t = {}
        soft_t = {}

        def turn_inputs(dh):
            beta_t[dh] = bank(OUT_BANKS[0], [P, 2, PACK, P], BF16, "beta_t")
            for z in (REAL, IMAG):
                for t in range(PACK):
                    nc.tensor.transpose(beta_t[dh][:, z, t, :], beta_bf[:, z, t, dh * P : (dh + 1) * P], ident_bf[:])
            soft_t[dh] = turn_f32(soft, dh, OUT_BANKS[1], "soft_t")

        recip = {}

        def make_recip(dh):
            recip[dh] = keep.tile([P, PACK, P], F32, name="recip%d" % dh)
            nc.scalar.activation(out=recip[dh][:], in_=log_den_t[dh][:], func=ACT.Exp, scale=-1.0)

        gain = {}

        def make_gain(dh, z):
            tile = keep.tile([P, M], F32, name="gain%d%d" % (dh, z))
            nc.vector.tensor_tensor(
                out=stored(tile[:], z == IMAG),
                in0=walked(beta_t[dh][:, z, :, :], z == IMAG),
                in1=walked(recip[dh][:], z == IMAG),
                op=ALU.mult,
            )
            gain[(dh, z)] = tile

        def make_coef_soft(dh, z):
            tile = keep.tile([P, M], F32, name="coef%d%d%d" % (dh, z, z))
            nc.vector.tensor_tensor(
                out=stored(tile[:], z == IMAG),
                in0=walked(soft_t[dh][:], z == IMAG),
                in1=stored(gain[(dh, z)][:], z == IMAG),
                op=ALU.mult,
            )
            coef[(dh, z, z)] = tile

        def make_coef_omega(dh, z):
            tile = keep.tile([P, M], F32, name="coef%d%d%d" % (dh, z, 1 - z))
            nc.gpsimd.tensor_tensor(out=tile[:], in0=gain[(dh, z)][:], in1=w_rows[:, z, :], op=ALU.mult)
            coef[(dh, z, 1 - z)] = tile

        exp_a = keep.tile([P, PACK, D], F32, name="exp_a")
        for pair in slot_pairs:
            nc.scalar.activation(out=exp_a[:, pair, :], in_=a_bf[:, pair, :], func=ACT.Exp)
        widen(0, True, range(PLANES))
        w_sq = keep.tile([P, PACK], F32, name="w_sq")
        nc.vector.tensor_tensor(out=w_sq[:], in0=w_bf[:], in1=w_bf[:], op=ALU.mult)
        w_neg = keep.tile([P, PACK], BF16, name="w_neg")
        nc.vector.tensor_scalar(out=w_neg[:], in0=w_bf[:], scalar1=-1.0, scalar2=None, op0=ALU.mult)
        w_acc = bank(OMEGA_BANK, [P, 2, PACK, P], BF16, "w_acc")
        for z, signed in ((REAL, w_bf), (IMAG, w_neg)):
            for t in range(PACK):
                column = signed[:, t : t + 1].to_broadcast([P, P])
                nc.tensor.matmul(out=w_acc[:, z, t, :], lhsT=column, rhs=ident_bf[:], start=True, stop=True)

        log_a = keep.tile([P, PACK, D], F32, name="log_a")
        for t in range(PACK):
            nc.scalar.activation(out=log_a[:, t, :], in_=exp_a[:, t, :], func=ACT.Ln, bias=1.0)

        widen(1, True, range(EARLY_PLANES))
        soft = keep.tile([P, PACK, D], F32, name="soft")
        soft_sq = keep.tile([P, PACK, D], F32, name="soft_sq")
        log_den = keep.tile([P, PACK, D], F32, name="log_den")
        for t in range(PACK):
            nc.vector.scalar_tensor_tensor(
                out=soft[:, t, :], in0=log_a[:, t, :], scalar=LOG_CAP, in1=a_bf[:, t, :], op0=ALU.min, op1=ALU.max
            )
        for t in range(PACK):
            if t < SQUARES_ON_SCALAR:
                nc.scalar.activation(out=soft_sq[:, t, :], in_=soft[:, t, :], func=ACT.Square)
            else:
                nc.vector.tensor_tensor(out=soft_sq[:, t, :], in0=soft[:, t, :], in1=soft[:, t, :], op=ALU.mult)
        for t in range(PACK):
            nc.scalar.activation(out=log_den[:, t, :], in_=soft_sq[:, t, :], func=ACT.Ln, bias=w_sq[:, t : t + 1])
        widen(1, True, range(EARLY_PLANES, PLANES))
        interleave(0, nc.vector.tensor_copy)
        interleave(1, nc.vector.tensor_copy)
        quantize_v(0)
        quantize_v(1)
        turn_inputs(0)
        log_den_t = [turn_f32(log_den, dh, Z_BANK + dh, "log_den_t") for dh in range(HALVES)]
        keep_warm(OMEGA_BANK - 1, WARM_LONG)
        encode(0)

        make_recip(0)
        w_rows = keep.tile([P, 2, M], BF16, name="w_rows")
        for z in (REAL, IMAG):
            nc.scalar.copy(out=stored(w_rows[:, z, :], z == IMAG), in_=walked(w_acc[:, z, :, :], z == IMAG))
        make_recip(1)
        widen(2, False, range(PLANES))
        interleave(2, nc.scalar.copy)
        widen(3, False, range(PLANES))

        for z in (IMAG, REAL):
            make_gain(0, z)
            make_coef_omega(0, z)
        encode(1)
        make_coef_soft(0, IMAG)
        make_coef_soft(0, REAL)
        product(0, IMAG, IMAG)
        turn_inputs(1)
        keep_warm(Z_BANK + IMAG, WARM_LONG)
        product(0, IMAG, REAL)
        add_terms(0, IMAG, nc.gpsimd)
        product(0, REAL, REAL)
        product(0, REAL, IMAG)

        for j in range(1, COUNT + 1):
            if j < COUNT:
                product(j, IMAG, REAL)
            if j - 1 in REAL_AS_PAIRS:
                add_terms(j - 1, REAL, nc.vector)
            if j >= 2:
                quantize_z(j - 2)
            if j <= AHEAD_FROM:
                quantize_v(j + 1)
            if AHEAD_FROM <= j < COUNT - 2:
                quantize_v(j + 2)
            if j < COUNT:
                product(j, IMAG, IMAG)
                add_terms(j, IMAG, nc.gpsimd)
                if j == 1:
                    make_gain(1, IMAG)
                    make_coef_omega(1, IMAG)
                    make_gain(1, REAL)
                if j == 2:
                    make_coef_omega(1, REAL)
                    make_coef_soft(1, IMAG)
                    make_coef_soft(1, REAL)
                product(j, REAL, REAL)
                product(j, REAL, IMAG)
            if j == 2:
                keep_warm(OUT_BANKS[0], WARM_LONG)
            turn_z(j - 1, nc.vector.tensor_copy if j == COUNT else nc.scalar.copy)
            if j in (2, 3):
                keep_warm(OUT_BANKS[0], WARM_SHORT)
            if j + 1 < COUNT:
                encode(j + 1)
            if j < AHEAD_FROM:
                interleave(j + 2, nc.scalar.copy)
            if AHEAD_FROM - 1 <= j < COUNT - 3:
                interleave(j + 3, nc.scalar.copy)
            if j >= 2:
                decode(j - 2, LATE_OUT_BANKS[0] if j == COUNT else OUT_BANKS, (nc.scalar.copy,))
        quantize_z(COUNT - 1)
        decode(COUNT - 1, LATE_OUT_BANKS[1], (nc.vector.tensor_copy, nc.scalar.copy))
